import numpy as np
import ml_dtypes


def mxq(x, axis, fmt="e4m3"):
    dtype, down = {"e4m3": (ml_dtypes.float8_e4m3fn, 7), "e5m2": (ml_dtypes.float8_e5m2, 14)}[fmt]
    v = np.moveaxis(np.asarray(x, np.float32).astype(ml_dtypes.bfloat16).astype(np.float64), axis, -1)
    blocks = v.reshape(v.shape[:-1] + (-1, 32))
    amax = np.abs(blocks).max(-1, keepdims=True)
    byte = np.maximum(np.where(amax > 0, np.frexp(amax)[1] - 1 + 127, 0) - down, 1)
    scale = np.exp2(byte - 127.0)
    codes = (blocks / scale).astype(np.float32).astype(dtype).astype(np.float64)
    return np.moveaxis((codes * scale).reshape(v.shape), -1, axis)


WIDE = False


def mx_kscale(k):
    if not WIDE:
        return np.ones(k)
    levels = np.array([10, -10, 5, -5, 0])
    if k % 512:
        return np.exp2(np.random.permutation(np.resize(levels, k // 32))).repeat(32)
    a = np.empty((k // 512, 16))
    for p in range(k // 512):
        a[p, :8] = np.random.permutation(np.resize(levels, 8))
        for g in range(8):
            far = levels[np.abs(levels - a[p, g]) >= 10]
            a[p, g + 8] = far[np.random.randint(len(far))]
    return np.exp2(a.ravel()).repeat(32)


def f64(x):
    return np.asarray(x).astype(np.float64)


def striped(idx):
    return np.tile(idx.reshape(-1, 16).T, (8, 1)).astype(np.uint16)


def unstriped(offs):
    return offs[:16].T.reshape(-1).astype(np.int64)


def pack_weight(w):
    k, n = w.shape
    w = f64(np.asarray(w, np.float32).astype(ml_dtypes.bfloat16)).reshape(k // 32, 32, n)
    amax = np.abs(w).max(1)
    byte = np.clip(np.where(amax > 0, np.frexp(amax)[1] - 1 + 127 - 7, 1), 1, 254)
    scaled = (w * np.exp2(127.0 - byte)[:, None, :]).reshape(k, n).astype(np.float32)
    words = np.ascontiguousarray(scaled.reshape(k // 512, 128, 4, n).transpose(0, 1, 3, 2)).astype(ml_dtypes.float8_e4m3fn).view(np.uint8)
    return words, np.ascontiguousarray(byte.astype(np.uint8).reshape(k // 512, 16, n))


def unpack_weight(words, scales):
    g, p, n, _ = words.shape
    vals = np.ascontiguousarray(words).view(ml_dtypes.float8_e4m3fn).astype(np.float64) * np.repeat(np.exp2(scales.astype(np.float64) - 127.0), 8, axis=1)[..., None]
    return vals.transpose(0, 1, 3, 2).reshape(g * 512, n)


def relu(v):
    return np.maximum(v, 0.0)


K, T, S, H, N, U = 512, 2048, 512, 512, 256, 1024


def setup_inputs():
    n = np.random.standard_normal
    s = mx_kscale(K)[:, None]
    u = mx_kscale(H)
    packed_w2 = pack_weight(n((H, N)) / np.sqrt(H) / u[:, None])
    return {
        "xT": (n((K, T)) * s).astype(np.float32),
        "w1": (n((K, H)) / np.sqrt(K) / s * u).astype(np.float32),
        "w2_words": packed_w2[0],
        "w2_scales": packed_w2[1],
        "skip": (n((H, U)) * u[:, None]).astype(np.float32),
        "offs": striped(np.random.permutation(T)[:S]),
        "cell": striped(np.random.permutation(U)[:S]),
    }


def reference(xT, w1, w2_words, w2_scales, skip, offs, cell):
    xq = mxq(f64(xT)[:, unstriped(offs)], 0, "e4m3")
    up = np.zeros((H, U))
    up[:, unstriped(cell)] = relu(mxq(f64(w1), 0, "e4m3").T @ xq)
    z = up + f64(skip)
    return unpack_weight(w2_words, w2_scales).T @ mxq(z, 0, "e4m3")

@@ -1,0 +1,179 @@
+from contextlib import ExitStack
+
+import concourse.mybir as mybir
+
+K, T, S, H, N, U = 512, 2048, 512, 512, 256, 1024
+FLOPS = 2 * K * H * S + 2 * H * N * U
+
+F32 = mybir.dt.float32
+BF16 = mybir.dt.bfloat16
+I32 = mybir.dt.int32
+U32 = mybir.dt.uint32
+U16 = mybir.dt.uint16
+U8 = mybir.dt.uint8
+FP8X4 = mybir.dt.float8_e4m3fn_x4
+ADD = mybir.AluOpType.add
+RELU = mybir.ActivationFunctionType.Relu
+
+P = 128
+PACK = 4
+LIST_ROWS = 16
+HALF = S // 2
+GROUP = 256
+CHUNKS = (128, 128, 128, 128, 256, 256)
+WEAVE_ON_VECTOR = (5,)
+SPLIT_EXIT = (4, 5)
+
+
+def tile_picked_unet_relu_e_kernel(tc, xT, w1, w2_words, w2_scales, skip, offs, cell, out):
+    nc = tc.nc
+    with ExitStack() as ctx:
+        keep = ctx.enter_context(tc.tile_pool(name="keep", bufs=1))
+        psum = ctx.enter_context(tc.psum_pool(name="psum", bufs=8))
+
+        offs_sb = keep.tile([P, S // LIST_ROWS], U16, name="offs_sb")
+        cell_sb = keep.tile([P, S // LIST_ROWS], U16, name="cell_sb")
+        x_rows = [keep.tile([P, T], F32, name="x_rows%d" % j) for j in range(PACK)]
+        w1_rows = [keep.tile([P, 2, H], F32, name="w1_rows%d" % u) for u in range(2)]
+        groups = [slice(g, g + GROUP) for g in range(0, U, GROUP)]
+        skip_even = [keep.tile([P, 2, GROUP], F32, name="skip_even%d" % g, align_bytes=64) for g in range(len(groups))]
+        skip_odd = [keep.tile([P, U], F32, name="skip_odd%d" % u) for u in range(2)]
+        up = [keep.tile([P, U], F32, name="up%d" % t) for t in range(PACK)]
+        w2_codes = keep.tile([P, N], U32, name="w2_codes", align_bytes=64)
+        w2_plane = keep.tile([P, N], U8, name="w2_plane", align_bytes=64)
+
+        x_by_slot = xT.rearrange("(p j) c -> p j c", j=PACK)
+        w1_by_slot = w1.rearrange("(p j) c -> p j c", j=PACK)
+        skip_by_slot = skip.rearrange("(p u e) v -> p e u v", u=2, e=2)
+
+        nc.sync.dma_start(out=x_rows[0][:], in_=x_by_slot[:, 0, :])
+        nc.sync.dma_start(offs_sb[:], offs)
+        for j in range(1, PACK):
+            nc.sync.dma_start(out=x_rows[j][:], in_=x_by_slot[:, j, :])
+        nc.sync.dma_start(cell_sb[:], cell)
+        for u in range(2):
+            nc.sync.dma_start(out=w1_rows[u][:], in_=w1_by_slot[:, 2 * u : 2 * u + 2, :])
+        for g, cols in enumerate(groups):
+            nc.sync.dma_start(out=skip_even[g][:], in_=skip_by_slot[:, 0, :, cols])
+        for u in range(2):
+            nc.sync.dma_start(out=skip_odd[u][:], in_=skip_by_slot[:, 1, u, :])
+        nc.sync.dma_start(out=w2_codes[:].bitcast(I32), in_=w2_words[0].rearrange("p n t -> p (n t)").bitcast(I32))
+        nc.vector.memset(w2_plane[:].bitcast(I32), 0)
+        for q in range(4):
+            nc.sync.dma_start(out=w2_plane[32 * q : 32 * q + 4, :].bitcast(I32), in_=w2_scales[0, 4 * q : 4 * q + 4, :].bitcast(I32))
+
+        for t in range(PACK):
+            nc.vector.memset(up[t][:], 0.0)
+
+        picked = keep.tile([P, S, PACK], BF16, name="picked", align_bytes=64)
+        for j in range(PACK - 1):
+            nc.vector.tensor_copy(picked[:, :, j], x_rows[j][:].indirect(offs_sb[:]))
+        halves = [slice(0, HALF), slice(HALF, S)]
+        list_halves = [slice(0, HALF // LIST_ROWS), slice(HALF // LIST_ROWS, S // LIST_ROWS)]
+        for a in range(2):
+            nc.vector.tensor_copy(picked[:, halves[a], PACK - 1], x_rows[PACK - 1][:].indirect(offs_sb[:, list_halves[a]]))
+        x_codes = keep.tile([P, S], U32, name="x_codes", align_bytes=64)
+        x_plane = keep.tile([P, S], U8, name="x_plane", align_bytes=64)
+        for a in range(2):
+            nc.vector.quantize_mx(out=x_codes[:, halves[a]].bitcast(FP8X4), scales=x_plane[:, halves[a]],
+                                  in_=picked[:, halves[a], :].rearrange("p s j -> p (s j)"))
+
+        w1_bf = [keep.tile([P, P, PACK], BF16, name="w1_bf%d" % t, align_bytes=64) for t in range(PACK)]
+        w1_codes = [keep.tile([P, P], U32, name="w1_codes%d" % t, align_bytes=64) for t in range(PACK)]
+        w1_plane = [keep.tile([P, P], U8, name="w1_plane%d" % t, align_bytes=64) for t in range(PACK)]
+        hidden = [keep.tile([P, S], F32, name="hidden%d" % t) for t in range(PACK)]
+
+        def deal_w1(t, u):
+            nc.scalar.copy(w1_bf[t][:, :, 2 * u : 2 * u + 2],
+                           w1_rows[u][:].rearrange("p j (m t) -> p t m j", t=PACK)[:, t, :, :])
+
+        def quantize_w1(t):
+            nc.vector.quantize_mx(out=w1_codes[t][:].bitcast(FP8X4), scales=w1_plane[t][:],
+                                  in_=w1_bf[t][:].rearrange("p m j -> p (m j)"))
+
+        def first_layer(t, cols, on_vector=False):
+            acc = psum.tile([P, 512], F32, name="acc")
+            width = cols.stop - cols.start
+            nc.tensor.matmul_mx(out=acc[:, :width], lhsT=w1_codes[t][:].bitcast(FP8X4), lhsT_scale=w1_plane[t][:],
+                                rhs=x_codes[:, cols].bitcast(FP8X4), rhs_scale=x_plane[:, cols], start=True, stop=True)
+            if on_vector:
+                nc.vector.tensor_scalar_max(hidden[t][:, cols], acc[:, :width], 0.0)
+            else:
+                nc.scalar.activation(hidden[t][:, cols], acc[:, :width], RELU)
+
+        def scatter(t, cols):
+            entries = cell_sb[:, cols.start // LIST_ROWS : cols.stop // LIST_ROWS]
+            nc.vector.tensor_copy(up[t][:].indirect(entries), hidden[t][:, cols])
+
+        def add_skip(t, engine):
+            u, e = divmod(t, 2)
+            for g, cols in enumerate(groups):
+                source = skip_odd[u][:, cols] if e else skip_even[g][:, u, :]
+                halves_of_words = skip_even[g][:, u, :].bitcast(BF16).rearrange("p (v e) -> p v e", e=2)
+                engine.tensor_tensor(halves_of_words[:, :, e], up[t][:, cols], source, ADD)
+
+        deal_w1(0, 0)
+        deal_w1(1, 0)
+        deal_w1(0, 1)
+        quantize_w1(0)
+        deal_w1(1, 1)
+        first_layer(0, halves[0], on_vector=True)
+        first_layer(0, halves[1])
+        scatter(0, halves[0])
+        quantize_w1(1)
+        scatter(0, halves[1])
+        for t in (2, 3):
+            deal_w1(t, 0)
+            deal_w1(t, 1)
+        whole = slice(0, S)
+        first_layer(1, whole)
+        add_skip(0, nc.gpsimd)
+        for t in (1, 2, 3):
+            if t < 3:
+                quantize_w1(t + 1)
+                first_layer(t + 1, whole)
+            scatter(t, whole)
+            add_skip(t, nc.gpsimd if t < 3 else nc.vector)
+
+        out_by_tile = out.rearrange("(a p) v -> p a v", p=P)
+        spans = []
+        start = 0
+        for width in CHUNKS:
+            spans.append(slice(start, start + width))
+            start = start + width
+        for c, cols in enumerate(spans):
+            width = cols.stop - cols.start
+            g, first = divmod(cols.start, GROUP)
+            z = keep.tile([P, width, 2], I32, name="z%d" % c, align_bytes=64)
+            pair_rows = skip_even[g][:, :, first : first + width]
+            if c in WEAVE_ON_VECTOR:
+                nc.vector.tensor_copy(z[:], pair_rows.bitcast(I32).rearrange("p u v -> p v u"))
+            else:
+                nc.scalar.copy(z[:].bitcast(U32), pair_rows.bitcast(U32).rearrange("p u v -> p v u"))
+            z_codes = keep.tile([P, width], U32, name="z_codes%d" % c, align_bytes=64)
+            z_plane = keep.tile([P, width], U8, name="z_plane%d" % c, align_bytes=64)
+            nc.vector.quantize_mx(out=z_codes[:].bitcast(FP8X4), scales=z_plane[:],
+                                  in_=z[:].rearrange("p v u -> p (v u)").bitcast(BF16))
+
+            def second_layer(acc, a):
+                nc.tensor.matmul_mx(out=acc, lhsT=w2_codes[:, a * P : (a + 1) * P].bitcast(FP8X4),
+                                    lhsT_scale=w2_plane[:, a * P : (a + 1) * P], rhs=z_codes[:].bitcast(FP8X4), rhs_scale=z_plane[:],
+                                    start=True, stop=True)
+
+            if c in SPLIT_EXIT:
+                for a in range(N // P):
+                    acc = psum.tile([P, 512], F32, name="acc")
+                    second_layer(acc[:, :width], a)
+                    result = keep.tile([P, width], F32, name="result%d_%d" % (c, a))
+                    if a == 0:
+                        nc.scalar.copy(result[:], acc[:, :width])
+                    else:
+                        nc.vector.tensor_copy(result[:], acc[:, :width])
+                    nc.sync.dma_start(out=out_by_tile[:, a, cols], in_=result[:])
+            else:
+                acc = psum.tile([P, 512], F32, name="acc")
+                for a in range(N // P):
+                    second_layer(acc[:, a * width : (a + 1) * width], a)
+                result = keep.tile([P, N // P, width], F32, name="result%d" % c)
+                nc.scalar.copy(result[:].rearrange("p a v -> p (a v)"), acc[:, : 2 * width])
+                nc.sync.dma_start(out=out_by_tile[:, :, cols], in_=result[:])

@@ -20,6 +20,7 @@ PACK = 4
 LIST_ROWS = 16
 HALF = S // 2
 GROUP = 256
+ADD_CUT = 640
 CHUNKS = (128, 128, 128, 128, 256, 256)
 WEAVE_ON_VECTOR = (5,)
 SPLIT_EXIT = (4, 5)
@@ -36,27 +37,26 @@ def tile_picked_unet_relu_e_kernel(tc, xT, w1, w2_words, w2_scales, skip, offs, 
         x_rows = [keep.tile([P, T], F32, name="x_rows%d" % j) for j in range(PACK)]
         w1_rows = [keep.tile([P, 2, H], F32, name="w1_rows%d" % u) for u in range(2)]
         groups = [slice(g, g + GROUP) for g in range(0, U, GROUP)]
-        skip_even = [keep.tile([P, 2, GROUP], F32, name="skip_even%d" % g, align_bytes=64) for g in range(len(groups))]
-        skip_odd = [keep.tile([P, U], F32, name="skip_odd%d" % u) for u in range(2)]
+        skip01 = keep.tile([P, 2, U], F32, name="skip01")
+        pairs = [keep.tile([P, 2, GROUP], F32, name="pairs%d" % g, align_bytes=64) for g in range(len(groups))]
+        skip23 = keep.tile([P, 2, U], F32, name="skip23")
         up = [keep.tile([P, U], F32, name="up%d" % t) for t in range(PACK)]
         w2_codes = keep.tile([P, N], U32, name="w2_codes", align_bytes=64)
         w2_plane = keep.tile([P, N], U8, name="w2_plane", align_bytes=64)
 
         x_by_slot = xT.rearrange("(p j) c -> p j c", j=PACK)
         w1_by_slot = w1.rearrange("(p j) c -> p j c", j=PACK)
-        skip_by_slot = skip.rearrange("(p u e) v -> p e u v", u=2, e=2)
+        skip_by_slot = skip.rearrange("(p t) v -> p t v", t=PACK)
 
         nc.sync.dma_start(out=x_rows[0][:], in_=x_by_slot[:, 0, :])
         nc.sync.dma_start(offs_sb[:], offs)
         for j in range(1, PACK):
             nc.sync.dma_start(out=x_rows[j][:], in_=x_by_slot[:, j, :])
-        nc.sync.dma_start(cell_sb[:], cell)
         for u in range(2):
             nc.sync.dma_start(out=w1_rows[u][:], in_=w1_by_slot[:, 2 * u : 2 * u + 2, :])
-        for g, cols in enumerate(groups):
-            nc.sync.dma_start(out=skip_even[g][:], in_=skip_by_slot[:, 0, :, cols])
-        for u in range(2):
-            nc.sync.dma_start(out=skip_odd[u][:], in_=skip_by_slot[:, 1, u, :])
+        nc.sync.dma_start(cell_sb[:], cell)
+        nc.sync.dma_start(out=skip01[:], in_=skip_by_slot[:, 0:2, :])
+        nc.sync.dma_start(out=skip23[:], in_=skip_by_slot[:, 2:4, :])
         nc.sync.dma_start(out=w2_codes[:].bitcast(I32), in_=w2_words[0].rearrange("p n t -> p (n t)").bitcast(I32))
         nc.vector.memset(w2_plane[:].bitcast(I32), 0)
         for q in range(4):
@@ -78,23 +78,26 @@ def tile_picked_unet_relu_e_kernel(tc, xT, w1, w2_words, w2_scales, skip, offs, 
             nc.vector.quantize_mx(out=x_codes[:, halves[a]].bitcast(FP8X4), scales=x_plane[:, halves[a]],
                                   in_=picked[:, halves[a], :].rearrange("p s j -> p (s j)"))
 
-        w1_bf = [keep.tile([P, P, PACK], BF16, name="w1_bf%d" % t, align_bytes=64) for t in range(PACK)]
-        w1_codes = [keep.tile([P, P], U32, name="w1_codes%d" % t, align_bytes=64) for t in range(PACK)]
-        w1_plane = [keep.tile([P, P], U8, name="w1_plane%d" % t, align_bytes=64) for t in range(PACK)]
+        w1_parts = [slice(0, 1), slice(1, 2), slice(2, 4)]
+        w1_bf = [keep.tile([P, part.stop - part.start, P, PACK], BF16, name="w1_bf%d" % k, align_bytes=64) for k, part in enumerate(w1_parts)]
+        w1_codes = keep.tile([P, H], U32, name="w1_codes", align_bytes=64)
+        w1_plane = keep.tile([P, H], U8, name="w1_plane", align_bytes=64)
         hidden = [keep.tile([P, S], F32, name="hidden%d" % t) for t in range(PACK)]
 
-        def deal_w1(t, u):
-            nc.scalar.copy(w1_bf[t][:, :, 2 * u : 2 * u + 2],
-                           w1_rows[u][:].rearrange("p j (m t) -> p t m j", t=PACK)[:, t, :, :])
+        def deal_w1(copy, u, k):
+            copy(w1_bf[k][:, :, :, 2 * u : 2 * u + 2].rearrange("p t m j -> p m j t"),
+                 w1_rows[u][:].rearrange("p j (m t) -> p m j t", t=PACK)[:, :, :, w1_parts[k]])
 
-        def quantize_w1(t):
-            nc.vector.quantize_mx(out=w1_codes[t][:].bitcast(FP8X4), scales=w1_plane[t][:],
-                                  in_=w1_bf[t][:].rearrange("p m j -> p (m j)"))
+        def quantize_w1(k):
+            cols = slice(w1_parts[k].start * P, w1_parts[k].stop * P)
+            nc.vector.quantize_mx(out=w1_codes[:, cols].bitcast(FP8X4), scales=w1_plane[:, cols],
+                                  in_=w1_bf[k][:].rearrange("p t m j -> p (t m j)"))
 
         def first_layer(t, cols, on_vector=False):
             acc = psum.tile([P, 512], F32, name="acc")
             width = cols.stop - cols.start
-            nc.tensor.matmul_mx(out=acc[:, :width], lhsT=w1_codes[t][:].bitcast(FP8X4), lhsT_scale=w1_plane[t][:],
+            mine = slice(t * P, (t + 1) * P)
+            nc.tensor.matmul_mx(out=acc[:, :width], lhsT=w1_codes[:, mine].bitcast(FP8X4), lhsT_scale=w1_plane[:, mine],
                                 rhs=x_codes[:, cols].bitcast(FP8X4), rhs_scale=x_plane[:, cols], start=True, stop=True)
             if on_vector:
                 nc.vector.tensor_scalar_max(hidden[t][:, cols], acc[:, :width], 0.0)
@@ -105,35 +108,36 @@ def tile_picked_unet_relu_e_kernel(tc, xT, w1, w2_words, w2_scales, skip, offs, 
             entries = cell_sb[:, cols.start // LIST_ROWS : cols.stop // LIST_ROWS]
             nc.vector.tensor_copy(up[t][:].indirect(entries), hidden[t][:, cols])
 
-        def add_skip(t, engine):
-            u, e = divmod(t, 2)
-            for g, cols in enumerate(groups):
-                source = skip_odd[u][:, cols] if e else skip_even[g][:, u, :]
-                halves_of_words = skip_even[g][:, u, :].bitcast(BF16).rearrange("p (v e) -> p v e", e=2)
-                engine.tensor_tensor(halves_of_words[:, :, e], up[t][:, cols], source, ADD)
+        def word_halves(g, u):
+            return pairs[g][:, u, :].bitcast(BF16).rearrange("p (v e) -> p v e", e=2)
 
-        deal_w1(0, 0)
-        deal_w1(1, 0)
-        deal_w1(0, 1)
+        for k in range(len(w1_parts)):
+            deal_w1(nc.scalar.copy, 0, k)
+        deal_w1(nc.vector.tensor_copy, 1, 0)
+        deal_w1(nc.vector.tensor_copy, 1, 1)
         quantize_w1(0)
-        deal_w1(1, 1)
         first_layer(0, halves[0], on_vector=True)
         first_layer(0, halves[1])
-        scatter(0, halves[0])
+        deal_w1(nc.vector.tensor_copy, 1, 2)
         quantize_w1(1)
-        scatter(0, halves[1])
-        for t in (2, 3):
-            deal_w1(t, 0)
-            deal_w1(t, 1)
+        quantize_w1(2)
         whole = slice(0, S)
-        first_layer(1, whole)
-        add_skip(0, nc.gpsimd)
+        scatter(0, whole)
         for t in (1, 2, 3):
-            if t < 3:
-                quantize_w1(t + 1)
-                first_layer(t + 1, whole)
-            scatter(t, whole)
-            add_skip(t, nc.gpsimd if t < 3 else nc.vector)
+            first_layer(t, whole)
+        nc.gpsimd.tensor_tensor(skip01[:, 0, :], up[0][:], skip01[:, 0, :], ADD)
+        scatter(1, whole)
+        nc.gpsimd.tensor_tensor(skip01[:, 1, :], up[1][:], skip01[:, 1, :], ADD)
+        scatter(2, whole)
+        for g, cols in enumerate(groups):
+            nc.scalar.copy(word_halves(g, 0), skip01[:, :, cols].rearrange("p e v -> p v e"))
+        for cols in (slice(0, ADD_CUT), slice(ADD_CUT, U)):
+            nc.gpsimd.tensor_tensor(skip23[:, 0, cols], up[2][:, cols], skip23[:, 0, cols], ADD)
+        for g, cols in enumerate(groups):
+            nc.scalar.copy(word_halves(g, 1), skip23[:, :, cols].rearrange("p e v -> p v e"))
+        scatter(3, whole)
+        for g, cols in enumerate(groups):
+            nc.vector.tensor_tensor(word_halves(g, 1)[:, :, 1], up[3][:, cols], skip23[:, 1, cols], ADD)
 
         out_by_tile = out.rearrange("(a p) v -> p a v", p=P)
         spans = []
@@ -145,7 +149,7 @@ def tile_picked_unet_relu_e_kernel(tc, xT, w1, w2_words, w2_scales, skip, offs, 
             width = cols.stop - cols.start
             g, first = divmod(cols.start, GROUP)
             z = keep.tile([P, width, 2], I32, name="z%d" % c, align_bytes=64)
-            pair_rows = skip_even[g][:, :, first : first + width]
+            pair_rows = pairs[g][:, :, first : first + width]
             if c in WEAVE_ON_VECTOR:
                 nc.vector.tensor_copy(z[:], pair_rows.bitcast(I32).rearrange("p u v -> p v u"))
             else:

@@ -1,6 +1,7 @@
 from contextlib import ExitStack
 
 import concourse.mybir as mybir
+from concourse.masks import make_identity
 
 K, T, S, H, N, U = 512, 2048, 512, 512, 256, 1024
 FLOPS = 2 * K * H * S + 2 * H * N * U
@@ -17,32 +18,47 @@ RELU = mybir.ActivationFunctionType.Relu
 
 P = 128
 PACK = 4
+BANK = 512
 LIST_ROWS = 16
 HALF = S // 2
-GROUP = 256
-ADD_CUT = 640
-CHUNKS = (128, 128, 128, 128, 256, 256)
-WEAVE_ON_VECTOR = (5,)
-SPLIT_EXIT = (4, 5)
+LEAD = 128
+GROUP = 128
+ORDER = (2, 0, 1, 3)
+VECTOR_CELLS = 640
+STAGED = (128, 512)
+ADD_PIECES = (128, 128, 256, 128)
+CHUNKS = (128, 128, 256, 256, 256)
+WEAVE_ON_VECTOR = (4,)
+SPLIT_EXIT = (2, 3, 4)
+CHUNK_ORDER = (0, 1, 2, 4, 3)
+
+
+def spans_of(widths):
+    spans = []
+    start = 0
+    for width in widths:
+        spans.append(slice(start, start + width))
+        start = start + width
+    return spans
 
 
 def tile_picked_unet_relu_e_kernel(tc, xT, w1, w2_words, w2_scales, skip, offs, cell, out):
     nc = tc.nc
     with ExitStack() as ctx:
         keep = ctx.enter_context(tc.tile_pool(name="keep", bufs=1))
-        psum = ctx.enter_context(tc.psum_pool(name="psum", bufs=8))
+        held = ctx.enter_context(tc.psum_pool(name="held", bufs=1))
+        psum = ctx.enter_context(tc.psum_pool(name="psum", bufs=6))
 
         offs_sb = keep.tile([P, S // LIST_ROWS], U16, name="offs_sb")
         cell_sb = keep.tile([P, S // LIST_ROWS], U16, name="cell_sb")
         x_rows = [keep.tile([P, T], F32, name="x_rows%d" % j) for j in range(PACK)]
         w1_rows = [keep.tile([P, 2, H], F32, name="w1_rows%d" % u) for u in range(2)]
-        groups = [slice(g, g + GROUP) for g in range(0, U, GROUP)]
-        skip01 = keep.tile([P, 2, U], F32, name="skip01")
-        pairs = [keep.tile([P, 2, GROUP], F32, name="pairs%d" % g, align_bytes=64) for g in range(len(groups))]
-        skip23 = keep.tile([P, 2, U], F32, name="skip23")
+        skip_rows = [keep.tile([P, 2, U], F32, name="skip_rows%d" % u) for u in range(2)]
+        pairs = keep.tile([P, U // GROUP, 2, GROUP], F32, name="pairs", align_bytes=64)
         up = [keep.tile([P, U], F32, name="up%d" % t) for t in range(PACK)]
         w2_codes = keep.tile([P, N], U32, name="w2_codes", align_bytes=64)
         w2_plane = keep.tile([P, N], U8, name="w2_plane", align_bytes=64)
+        ident = keep.tile([P, P], F32, name="ident")
 
         x_by_slot = xT.rearrange("(p j) c -> p j c", j=PACK)
         w1_by_slot = w1.rearrange("(p j) c -> p j c", j=PACK)
@@ -55,8 +71,8 @@ def tile_picked_unet_relu_e_kernel(tc, xT, w1, w2_words, w2_scales, skip, offs, 
         for u in range(2):
             nc.sync.dma_start(out=w1_rows[u][:], in_=w1_by_slot[:, 2 * u : 2 * u + 2, :])
         nc.sync.dma_start(cell_sb[:], cell)
-        nc.sync.dma_start(out=skip01[:], in_=skip_by_slot[:, 0:2, :])
-        nc.sync.dma_start(out=skip23[:], in_=skip_by_slot[:, 2:4, :])
+        for u in (1, 0):
+            nc.sync.dma_start(out=skip_rows[u][:], in_=skip_by_slot[:, 2 * u : 2 * u + 2, :])
         nc.sync.dma_start(out=w2_codes[:].bitcast(I32), in_=w2_words[0].rearrange("p n t -> p (n t)").bitcast(I32))
         nc.vector.memset(w2_plane[:].bitcast(I32), 0)
         for q in range(4):
@@ -64,100 +80,130 @@ def tile_picked_unet_relu_e_kernel(tc, xT, w1, w2_words, w2_scales, skip, offs, 
 
         for t in range(PACK):
             nc.vector.memset(up[t][:], 0.0)
+        make_identity(nc, ident[:])
 
         picked = keep.tile([P, S, PACK], BF16, name="picked", align_bytes=64)
         for j in range(PACK - 1):
             nc.vector.tensor_copy(picked[:, :, j], x_rows[j][:].indirect(offs_sb[:]))
-        halves = [slice(0, HALF), slice(HALF, S)]
-        list_halves = [slice(0, HALF // LIST_ROWS), slice(HALF // LIST_ROWS, S // LIST_ROWS)]
-        for a in range(2):
-            nc.vector.tensor_copy(picked[:, halves[a], PACK - 1], x_rows[PACK - 1][:].indirect(offs_sb[:, list_halves[a]]))
+        for first in (0, HALF):
+            nc.vector.tensor_copy(picked[:, first : first + HALF, PACK - 1],
+                                  x_rows[PACK - 1][:].indirect(offs_sb[:, first // LIST_ROWS : (first + HALF) // LIST_ROWS]))
         x_codes = keep.tile([P, S], U32, name="x_codes", align_bytes=64)
         x_plane = keep.tile([P, S], U8, name="x_plane", align_bytes=64)
-        for a in range(2):
-            nc.vector.quantize_mx(out=x_codes[:, halves[a]].bitcast(FP8X4), scales=x_plane[:, halves[a]],
-                                  in_=picked[:, halves[a], :].rearrange("p s j -> p (s j)"))
-
-        w1_parts = [slice(0, 1), slice(1, 2), slice(2, 4)]
-        w1_bf = [keep.tile([P, part.stop - part.start, P, PACK], BF16, name="w1_bf%d" % k, align_bytes=64) for k, part in enumerate(w1_parts)]
+        w1_bf = [keep.tile([P, P, PACK], BF16, name="w1_bf%d" % t, align_bytes=64) for t in range(PACK)]
         w1_codes = keep.tile([P, H], U32, name="w1_codes", align_bytes=64)
         w1_plane = keep.tile([P, H], U8, name="w1_plane", align_bytes=64)
         hidden = [keep.tile([P, S], F32, name="hidden%d" % t) for t in range(PACK)]
 
-        def deal_w1(copy, u, k):
-            copy(w1_bf[k][:, :, :, 2 * u : 2 * u + 2].rearrange("p t m j -> p m j t"),
-                 w1_rows[u][:].rearrange("p j (m t) -> p m j t", t=PACK)[:, :, :, w1_parts[k]])
+        def quantize_x(cols):
+            nc.vector.quantize_mx(out=x_codes[:, cols].bitcast(FP8X4), scales=x_plane[:, cols],
+                                  in_=picked[:, cols, :].rearrange("p s j -> p (s j)"))
 
-        def quantize_w1(k):
-            cols = slice(w1_parts[k].start * P, w1_parts[k].stop * P)
+        def deal_w1(copy, u, t):
+            copy(w1_bf[t][:, :, 2 * u : 2 * u + 2], w1_rows[u][:].rearrange("p j (m t) -> p m j t", t=PACK)[:, :, :, t])
+
+        def quantize_w1(t):
+            cols = slice(t * P, (t + 1) * P)
             nc.vector.quantize_mx(out=w1_codes[:, cols].bitcast(FP8X4), scales=w1_plane[:, cols],
-                                  in_=w1_bf[k][:].rearrange("p t m j -> p (t m j)"))
+                                  in_=w1_bf[t][:].rearrange("p m j -> p (m j)"))
 
-        def first_layer(t, cols, on_vector=False):
-            acc = psum.tile([P, 512], F32, name="acc")
+        def first_layer(t, cols):
+            acc = psum.tile([P, BANK], F32, name="acc")
             width = cols.stop - cols.start
             mine = slice(t * P, (t + 1) * P)
             nc.tensor.matmul_mx(out=acc[:, :width], lhsT=w1_codes[:, mine].bitcast(FP8X4), lhsT_scale=w1_plane[:, mine],
                                 rhs=x_codes[:, cols].bitcast(FP8X4), rhs_scale=x_plane[:, cols], start=True, stop=True)
-            if on_vector:
-                nc.vector.tensor_scalar_max(hidden[t][:, cols], acc[:, :width], 0.0)
-            else:
-                nc.scalar.activation(hidden[t][:, cols], acc[:, :width], RELU)
+            nc.scalar.activation(hidden[t][:, cols], acc[:, :width], RELU)
 
         def scatter(t, cols):
             entries = cell_sb[:, cols.start // LIST_ROWS : cols.stop // LIST_ROWS]
             nc.vector.tensor_copy(up[t][:].indirect(entries), hidden[t][:, cols])
 
-        def word_halves(g, u):
-            return pairs[g][:, u, :].bitcast(BF16).rearrange("p (v e) -> p v e", e=2)
+        def by_group(ap):
+            return ap.rearrange("p (g v) -> p g v", v=GROUP)
 
-        for k in range(len(w1_parts)):
-            deal_w1(nc.scalar.copy, 0, k)
-        deal_w1(nc.vector.tensor_copy, 1, 0)
-        deal_w1(nc.vector.tensor_copy, 1, 1)
-        quantize_w1(0)
-        first_layer(0, halves[0], on_vector=True)
-        first_layer(0, halves[1])
-        deal_w1(nc.vector.tensor_copy, 1, 2)
-        quantize_w1(1)
-        quantize_w1(2)
+        def slot_halves(t, cols):
+            words = pairs[:, cols.start // GROUP : cols.stop // GROUP, t // 2, :]
+            return words.bitcast(BF16).rearrange("p g (v e) -> p g v e", e=2)[:, :, :, t % 2]
+
+        def fill_words(u):
+            words = pairs[:, :, u, :].bitcast(BF16).rearrange("p g (v e) -> p g v e", e=2)
+            nc.scalar.copy(words, skip_rows[u][:].rearrange("p e (g v) -> p g v e", v=GROUP))
+
+        lead = slice(0, LEAD)
+        second = slice(LEAD, HALF)
+        late = slice(HALF, S)
+        rest = slice(LEAD, S)
         whole = slice(0, S)
-        scatter(0, whole)
-        for t in (1, 2, 3):
+        s0, s1, s2, s3 = ORDER
+
+        for t in ORDER:
+            deal_w1(nc.scalar.copy, 0, t)
+        quantize_x(lead)
+        quantize_x(second)
+        deal_w1(nc.vector.tensor_copy, 1, s0)
+        deal_w1(nc.scalar.copy, 1, s3)
+        quantize_w1(s0)
+        first_layer(s0, lead)
+        quantize_x(late)
+        deal_w1(nc.vector.tensor_copy, 1, s1)
+        deal_w1(nc.vector.tensor_copy, 1, s2)
+        quantize_w1(s1)
+        first_layer(s1, lead)
+        quantize_w1(s2)
+        quantize_w1(s3)
+        for t in (s0, s1):
+            first_layer(t, second)
+            first_layer(t, late)
+        scatter(s0, lead)
+        scatter(s1, lead)
+        scatter(s0, rest)
+        for t in (s2, s3):
             first_layer(t, whole)
-        nc.gpsimd.tensor_tensor(skip01[:, 0, :], up[0][:], skip01[:, 0, :], ADD)
-        scatter(1, whole)
-        nc.gpsimd.tensor_tensor(skip01[:, 1, :], up[1][:], skip01[:, 1, :], ADD)
-        scatter(2, whole)
-        for g, cols in enumerate(groups):
-            nc.scalar.copy(word_halves(g, 0), skip01[:, :, cols].rearrange("p e v -> p v e"))
-        for cols in (slice(0, ADD_CUT), slice(ADD_CUT, U)):
-            nc.gpsimd.tensor_tensor(skip23[:, 0, cols], up[2][:, cols], skip23[:, 0, cols], ADD)
-        for g, cols in enumerate(groups):
-            nc.scalar.copy(word_halves(g, 1), skip23[:, :, cols].rearrange("p e v -> p v e"))
-        scatter(3, whole)
-        for g, cols in enumerate(groups):
-            nc.vector.tensor_tensor(word_halves(g, 1)[:, :, 1], up[3][:, cols], skip23[:, 1, cols], ADD)
+        nc.gpsimd.tensor_tensor(skip_rows[1][:, 0, :], up[2][:], skip_rows[1][:, 0, :], ADD)
+        scatter(s1, rest)
+
+        turned = keep.tile([P, VECTOR_CELLS], F32, name="turned")
+        staged = []
+        for cols in spans_of(STAGED):
+            width = cols.stop - cols.start
+            there = psum.tile([P, BANK], F32, name="acc")
+            for v in range(0, width, P):
+                nc.tensor.transpose(there[:, v : v + P], skip_rows[1][:, 1, cols.start + v : cols.start + v + P], ident[:])
+            nc.scalar.copy(turned[:, cols], there[:, :width])
+            back = held.tile([P, BANK], F32, name="staged%d" % len(staged))
+            for v in range(0, width, P):
+                nc.tensor.transpose(back[:, v : v + P], turned[:, cols.start + v : cols.start + v + P], ident[:])
+            staged.append(back)
+
+        fill_words(1)
+        cells = slice(0, U)
+        nc.gpsimd.tensor_tensor(slot_halves(0, cells), by_group(up[0][:]), by_group(skip_rows[0][:, 0, :]), ADD)
+        scatter(s2, whole)
+        nc.gpsimd.tensor_tensor(slot_halves(1, cells), by_group(up[1][:]), by_group(skip_rows[0][:, 1, :]), ADD)
+        scatter(s3, whole)
+        for cols in spans_of(ADD_PIECES):
+            bank = 0 if cols.start < STAGED[0] else 1
+            first = cols.start - bank * STAGED[0]
+            nc.vector.tensor_tensor(slot_halves(3, cols), by_group(up[3][:, cols]),
+                                    by_group(staged[bank][:, first : first + cols.stop - cols.start]), ADD)
+        tail = slice(VECTOR_CELLS, U)
+        nc.gpsimd.tensor_tensor(slot_halves(3, tail), by_group(up[3][:, tail]), by_group(skip_rows[1][:, 1, tail]), ADD)
 
         out_by_tile = out.rearrange("(a p) v -> p a v", p=P)
-        spans = []
-        start = 0
-        for width in CHUNKS:
-            spans.append(slice(start, start + width))
-            start = start + width
-        for c, cols in enumerate(spans):
+        for c in CHUNK_ORDER:
+            cols = spans_of(CHUNKS)[c]
             width = cols.stop - cols.start
-            g, first = divmod(cols.start, GROUP)
-            z = keep.tile([P, width, 2], I32, name="z%d" % c, align_bytes=64)
-            pair_rows = pairs[g][:, :, first : first + width]
+            z = keep.tile([P, width // GROUP, GROUP, 2], I32, name="z%d" % c, align_bytes=64)
+            pair_rows = pairs[:, cols.start // GROUP : cols.stop // GROUP, :, :]
             if c in WEAVE_ON_VECTOR:
-                nc.vector.tensor_copy(z[:], pair_rows.bitcast(I32).rearrange("p u v -> p v u"))
+                nc.vector.tensor_copy(z[:], pair_rows.bitcast(I32).rearrange("p g u v -> p g v u"))
             else:
-                nc.scalar.copy(z[:].bitcast(U32), pair_rows.bitcast(U32).rearrange("p u v -> p v u"))
+                nc.scalar.copy(z[:].bitcast(U32), pair_rows.bitcast(U32).rearrange("p g u v -> p g v u"))
             z_codes = keep.tile([P, width], U32, name="z_codes%d" % c, align_bytes=64)
             z_plane = keep.tile([P, width], U8, name="z_plane%d" % c, align_bytes=64)
             nc.vector.quantize_mx(out=z_codes[:].bitcast(FP8X4), scales=z_plane[:],
-                                  in_=z[:].rearrange("p v u -> p (v u)").bitcast(BF16))
+                                  in_=z[:].rearrange("p g v u -> p (g v u)").bitcast(BF16))
 
             def second_layer(acc, a):
                 nc.tensor.matmul_mx(out=acc, lhsT=w2_codes[:, a * P : (a + 1) * P].bitcast(FP8X4),
@@ -166,7 +212,7 @@ def tile_picked_unet_relu_e_kernel(tc, xT, w1, w2_words, w2_scales, skip, offs, 
 
             if c in SPLIT_EXIT:
                 for a in range(N // P):
-                    acc = psum.tile([P, 512], F32, name="acc")
+                    acc = psum.tile([P, BANK], F32, name="acc")
                     second_layer(acc[:, :width], a)
                     result = keep.tile([P, width], F32, name="result%d_%d" % (c, a))
                     if a == 0:
@@ -175,7 +221,7 @@ def tile_picked_unet_relu_e_kernel(tc, xT, w1, w2_words, w2_scales, skip, offs, 
                         nc.vector.tensor_copy(result[:], acc[:, :width])
                     nc.sync.dma_start(out=out_by_tile[:, a, cols], in_=result[:])
             else:
-                acc = psum.tile([P, 512], F32, name="acc")
+                acc = psum.tile([P, BANK], F32, name="acc")
                 for a in range(N // P):
                     second_layer(acc[:, a * width : (a + 1) * width], a)
                 result = keep.tile([P, N // P, width], F32, name="result%d" % c)

@@ -90,7 +90,10 @@ def tile_picked_unet_relu_e_kernel(tc, xT, w1, w2_words, w2_scales, skip, offs, 
                                   x_rows[PACK - 1][:].indirect(offs_sb[:, first // LIST_ROWS : (first + HALF) // LIST_ROWS]))
         x_codes = keep.tile([P, S], U32, name="x_codes", align_bytes=64)
         x_plane = keep.tile([P, S], U8, name="x_plane", align_bytes=64)
-        w1_bf = [keep.tile([P, P, PACK], BF16, name="w1_bf%d" % t, align_bytes=64) for t in range(PACK)]
+        w1_low = keep.tile([P, 2, P, PACK], BF16, name="w1_low", align_bytes=64)
+        w1_first = keep.tile([P, P, PACK], BF16, name="w1_first", align_bytes=64)
+        w1_last = keep.tile([P, P, PACK], BF16, name="w1_last", align_bytes=64)
+        w1_bf = [w1_low[:, 0, :, :], w1_low[:, 1, :, :], w1_first[:], w1_last[:]]
         w1_codes = keep.tile([P, H], U32, name="w1_codes", align_bytes=64)
         w1_plane = keep.tile([P, H], U8, name="w1_plane", align_bytes=64)
         hidden = [keep.tile([P, S], F32, name="hidden%d" % t) for t in range(PACK)]
@@ -102,10 +105,14 @@ def tile_picked_unet_relu_e_kernel(tc, xT, w1, w2_words, w2_scales, skip, offs, 
         def deal_w1(copy, u, t):
             copy(w1_bf[t][:, :, 2 * u : 2 * u + 2], w1_rows[u][:].rearrange("p j (m t) -> p m j t", t=PACK)[:, :, :, t])
 
+        def deal_low(copy, u):
+            copy(w1_low[:, :, :, 2 * u : 2 * u + 2].rearrange("p t m j -> p m t j"),
+                 w1_rows[u][:].rearrange("p j (m t) -> p m t j", t=PACK)[:, :, 0:2, :])
+
         def quantize_w1(t):
             cols = slice(t * P, (t + 1) * P)
             nc.vector.quantize_mx(out=w1_codes[:, cols].bitcast(FP8X4), scales=w1_plane[:, cols],
-                                  in_=w1_bf[t][:].rearrange("p m j -> p (m j)"))
+                                  in_=w1_bf[t].rearrange("p m j -> p (m j)"))
 
         def first_layer(t, cols):
             acc = psum.tile([P, BANK], F32, name="acc")
@@ -137,8 +144,9 @@ def tile_picked_unet_relu_e_kernel(tc, xT, w1, w2_words, w2_scales, skip, offs, 
         whole = slice(0, S)
         s0, s1, s2, s3 = ORDER
 
-        for t in ORDER:
-            deal_w1(nc.scalar.copy, 0, t)
+        deal_w1(nc.scalar.copy, 0, s0)
+        deal_low(nc.scalar.copy, 0)
+        deal_w1(nc.scalar.copy, 0, s3)
         quantize_x(lead)
         quantize_x(second)
         deal_w1(nc.vector.tensor_copy, 1, s0)
@@ -146,8 +154,7 @@ def tile_picked_unet_relu_e_kernel(tc, xT, w1, w2_words, w2_scales, skip, offs, 
         quantize_w1(s0)
         first_layer(s0, lead)
         quantize_x(late)
-        deal_w1(nc.vector.tensor_copy, 1, s1)
-        deal_w1(nc.vector.tensor_copy, 1, s2)
+        deal_low(nc.vector.tensor_copy, 1)
         quantize_w1(s1)
         first_layer(s1, lead)
         quantize_w1(s2)

@@ -25,7 +25,7 @@ LEAD = 128
 GROUP = 128
 ORDER = (2, 0, 1, 3)
 VECTOR_CELLS = 640
-STAGED = (128, 512)
+STAGED = (512, 128)
 ADD_PIECES = (128, 128, 256, 128)
 CHUNKS = (128, 128, 256, 256, 256)
 WEAVE_ON_VECTOR = (4,)
@@ -47,15 +47,15 @@ def tile_picked_unet_relu_e_kernel(tc, xT, w1, w2_words, w2_scales, skip, offs, 
     with ExitStack() as ctx:
         keep = ctx.enter_context(tc.tile_pool(name="keep", bufs=1))
         held = ctx.enter_context(tc.psum_pool(name="held", bufs=1))
-        psum = ctx.enter_context(tc.psum_pool(name="psum", bufs=6))
+        psum = ctx.enter_context(tc.psum_pool(name="psum", bufs=5))
 
         offs_sb = keep.tile([P, S // LIST_ROWS], U16, name="offs_sb")
         cell_sb = keep.tile([P, S // LIST_ROWS], U16, name="cell_sb")
         x_rows = [keep.tile([P, T], F32, name="x_rows%d" % j) for j in range(PACK)]
         w1_rows = [keep.tile([P, 2, H], F32, name="w1_rows%d" % u) for u in range(2)]
         skip_rows = [keep.tile([P, 2, U], F32, name="skip_rows%d" % u) for u in range(2)]
-        pairs = keep.tile([P, U // GROUP, 2, GROUP], F32, name="pairs", align_bytes=64)
-        up = [keep.tile([P, U], F32, name="up%d" % t) for t in range(PACK)]
+        pairs = keep.tile([P, U // GROUP, 2, GROUP], F32, name="pairs", tag="pairs", align_bytes=64)
+        up = [keep.tile([P, U], F32, name="up%d" % t, tag="up%d" % t) for t in range(PACK)]
         w2_codes = keep.tile([P, N], U32, name="w2_codes", align_bytes=64)
         w2_plane = keep.tile([P, N], U8, name="w2_plane", align_bytes=64)
         ident = keep.tile([P, P], F32, name="ident")
@@ -170,24 +170,29 @@ def tile_picked_unet_relu_e_kernel(tc, xT, w1, w2_words, w2_scales, skip, offs, 
         nc.gpsimd.tensor_tensor(skip_rows[1][:, 0, :], up[2][:], skip_rows[1][:, 0, :], ADD)
         scatter(s1, rest)
 
-        turned = keep.tile([P, VECTOR_CELLS], F32, name="turned")
-        staged = []
-        for cols in spans_of(STAGED):
+        def stage_skip(cols, tag, there):
             width = cols.stop - cols.start
-            there = psum.tile([P, BANK], F32, name="acc")
             for v in range(0, width, P):
                 nc.tensor.transpose(there[:, v : v + P], skip_rows[1][:, 1, cols.start + v : cols.start + v + P], ident[:])
-            nc.scalar.copy(turned[:, cols], there[:, :width])
-            back = held.tile([P, BANK], F32, name="staged%d" % len(staged))
+            turned = keep.tile([P, width], F32, name="turned%d" % cols.start, tag=tag)
+            nc.scalar.copy(turned[:], there[:, :width])
+            back = held.tile([P, BANK], F32, name="staged%d" % cols.start, tag="staged%d" % (cols.start // BANK))
             for v in range(0, width, P):
-                nc.tensor.transpose(back[:, v : v + P], turned[:, cols.start + v : cols.start + v + P], ident[:])
-            staged.append(back)
+                nc.tensor.transpose(back[:, v : v + P], turned[:, v : v + P], ident[:])
+            return back
+
+        staged = [stage_skip(spans_of(STAGED)[0], "turned", psum.tile([P, BANK], F32, name="acc"))]
 
         fill_words(1)
         cells = slice(0, U)
         nc.gpsimd.tensor_tensor(slot_halves(0, cells), by_group(up[0][:]), by_group(skip_rows[0][:, 0, :]), ADD)
         scatter(s2, whole)
         nc.gpsimd.tensor_tensor(slot_halves(1, cells), by_group(up[1][:]), by_group(skip_rows[0][:, 1, :]), ADD)
+        staged.append(stage_skip(spans_of(STAGED)[1], "up1", held.tile([P, BANK], F32, name="there", tag="spare")))
+        warm = held.tile([P, BANK], F32, name="warm", tag="spare")
+        for a in range(N // P):
+            nc.tensor.matmul_mx(out=warm[:], lhsT=w2_codes[:, a * P : (a + 1) * P].bitcast(FP8X4), lhsT_scale=w2_plane[:, a * P : (a + 1) * P],
+                                rhs=x_codes[:].bitcast(FP8X4), rhs_scale=x_plane[:], start=True, stop=True)
         scatter(s3, whole)
         for cols in spans_of(ADD_PIECES):
             bank = 0 if cols.start < STAGED[0] else 1
@@ -198,39 +203,48 @@ def tile_picked_unet_relu_e_kernel(tc, xT, w1, w2_words, w2_scales, skip, offs, 
         nc.gpsimd.tensor_tensor(slot_halves(3, tail), by_group(up[3][:, tail]), by_group(skip_rows[1][:, 1, tail]), ADD)
 
         out_by_tile = out.rearrange("(a p) v -> p a v", p=P)
+        z_codes = {}
+        z_plane = {}
         for c in CHUNK_ORDER:
             cols = spans_of(CHUNKS)[c]
             width = cols.stop - cols.start
-            z = keep.tile([P, width // GROUP, GROUP, 2], I32, name="z%d" % c, align_bytes=64)
+            z = keep.tile([P, width // GROUP, GROUP, 2], I32, name="z%d" % c, tag="z0" if c in WEAVE_ON_VECTOR else "z%d" % c, align_bytes=64)
             pair_rows = pairs[:, cols.start // GROUP : cols.stop // GROUP, :, :]
             if c in WEAVE_ON_VECTOR:
                 nc.vector.tensor_copy(z[:], pair_rows.bitcast(I32).rearrange("p g u v -> p g v u"))
             else:
                 nc.scalar.copy(z[:].bitcast(U32), pair_rows.bitcast(U32).rearrange("p g u v -> p g v u"))
-            z_codes = keep.tile([P, width], U32, name="z_codes%d" % c, align_bytes=64)
-            z_plane = keep.tile([P, width], U8, name="z_plane%d" % c, align_bytes=64)
-            nc.vector.quantize_mx(out=z_codes[:].bitcast(FP8X4), scales=z_plane[:],
+            z_codes[c] = keep.tile([P, width], U32, name="z_codes%d" % c, align_bytes=64)
+            z_plane[c] = keep.tile([P, width], U8, name="z_plane%d" % c, align_bytes=64)
+            nc.vector.quantize_mx(out=z_codes[c][:].bitcast(FP8X4), scales=z_plane[c][:],
                                   in_=z[:].rearrange("p g v u -> p (g v u)").bitcast(BF16))
 
-            def second_layer(acc, a):
-                nc.tensor.matmul_mx(out=acc, lhsT=w2_codes[:, a * P : (a + 1) * P].bitcast(FP8X4),
-                                    lhsT_scale=w2_plane[:, a * P : (a + 1) * P], rhs=z_codes[:].bitcast(FP8X4), rhs_scale=z_plane[:],
-                                    start=True, stop=True)
+        def second_layer(acc, a, c):
+            nc.tensor.matmul_mx(out=acc, lhsT=w2_codes[:, a * P : (a + 1) * P].bitcast(FP8X4),
+                                lhsT_scale=w2_plane[:, a * P : (a + 1) * P], rhs=z_codes[c][:].bitcast(FP8X4), rhs_scale=z_plane[c][:],
+                                start=True, stop=True)
 
+        for c in CHUNK_ORDER:
+            cols = spans_of(CHUNKS)[c]
+            width = cols.stop - cols.start
             if c in SPLIT_EXIT:
                 for a in range(N // P):
-                    acc = psum.tile([P, BANK], F32, name="acc")
-                    second_layer(acc[:, :width], a)
-                    result = keep.tile([P, width], F32, name="result%d_%d" % (c, a))
+                    if c == CHUNK_ORDER[-1]:
+                        acc = held.tile([P, BANK], F32, name="last%d" % a, tag="staged%d" % a)
+                    else:
+                        acc = psum.tile([P, BANK], F32, name="acc")
+                    second_layer(acc[:, :width], a, c)
                     if a == 0:
+                        result = keep.tile([P, width], F32, name="result%d_0" % c)
                         nc.scalar.copy(result[:], acc[:, :width])
                     else:
+                        result = keep.tile([P, width], F32, name="result%d_1" % c, tag="z3" if c == SPLIT_EXIT[0] else "result%d_1" % c, align_bytes=64)
                         nc.vector.tensor_copy(result[:], acc[:, :width])
                     nc.sync.dma_start(out=out_by_tile[:, a, cols], in_=result[:])
             else:
-                acc = psum.tile([P, BANK], F32, name="acc")
+                acc = held.tile([P, BANK], F32, name="first", tag="spare") if c == 0 else psum.tile([P, BANK], F32, name="acc")
                 for a in range(N // P):
-                    second_layer(acc[:, a * width : (a + 1) * width], a)
-                result = keep.tile([P, N // P, width], F32, name="result%d" % c)
+                    second_layer(acc[:, a * width : (a + 1) * width], a, c)
+                result = keep.tile([P, N // P, width], F32, name="result%d" % c, tag="pairs" if c == 0 else "result%d" % c, align_bytes=64)
                 nc.scalar.copy(result[:].rearrange("p a v -> p (a v)"), acc[:, : 2 * width])
                 nc.sync.dma_start(out=out_by_tile[:, :, cols], in_=result[:])

@@ -189,10 +189,6 @@ def tile_picked_unet_relu_e_kernel(tc, xT, w1, w2_words, w2_scales, skip, offs, 
         scatter(s2, whole)
         nc.gpsimd.tensor_tensor(slot_halves(1, cells), by_group(up[1][:]), by_group(skip_rows[0][:, 1, :]), ADD)
         staged.append(stage_skip(spans_of(STAGED)[1], "up1", held.tile([P, BANK], F32, name="there", tag="spare")))
-        warm = held.tile([P, BANK], F32, name="warm", tag="spare")
-        for a in range(N // P):
-            nc.tensor.matmul_mx(out=warm[:], lhsT=w2_codes[:, a * P : (a + 1) * P].bitcast(FP8X4), lhsT_scale=w2_plane[:, a * P : (a + 1) * P],
-                                rhs=x_codes[:].bitcast(FP8X4), rhs_scale=x_plane[:], start=True, stop=True)
         scatter(s3, whole)
         for cols in spans_of(ADD_PIECES):
             bank = 0 if cols.start < STAGED[0] else 1

@@ -15,6 +15,7 @@ U8 = mybir.dt.uint8
 FP8X4 = mybir.dt.float8_e4m3fn_x4
 ADD = mybir.AluOpType.add
 RELU = mybir.ActivationFunctionType.Relu
+COPY = mybir.ActivationFunctionType.Copy
 
 P = 128
 PACK = 4
@@ -23,14 +24,10 @@ LIST_ROWS = 16
 HALF = S // 2
 LEAD = 128
 GROUP = 128
-ORDER = (2, 0, 1, 3)
-VECTOR_CELLS = 640
-STAGED = (512, 128)
-ADD_PIECES = (128, 128, 256, 128)
-CHUNKS = (128, 128, 256, 256, 256)
-WEAVE_ON_VECTOR = (4,)
-SPLIT_EXIT = (2, 3, 4)
-CHUNK_ORDER = (0, 1, 2, 4, 3)
+FRONT = 384
+DIRECT = 640
+CHUNKS = (128, 256, 256)
+TURNED = (U - DIRECT) // P
 
 
 def spans_of(widths):
@@ -46,19 +43,19 @@ def tile_picked_unet_relu_e_kernel(tc, xT, w1, w2_words, w2_scales, skip, offs, 
     nc = tc.nc
     with ExitStack() as ctx:
         keep = ctx.enter_context(tc.tile_pool(name="keep", bufs=1))
-        held = ctx.enter_context(tc.psum_pool(name="held", bufs=1))
-        psum = ctx.enter_context(tc.psum_pool(name="psum", bufs=5))
+        psum = ctx.enter_context(tc.psum_pool(name="psum", bufs=1))
 
         offs_sb = keep.tile([P, S // LIST_ROWS], U16, name="offs_sb")
         cell_sb = keep.tile([P, S // LIST_ROWS], U16, name="cell_sb")
         x_rows = [keep.tile([P, T], F32, name="x_rows%d" % j) for j in range(PACK)]
         w1_rows = [keep.tile([P, 2, H], F32, name="w1_rows%d" % u) for u in range(2)]
-        skip_rows = [keep.tile([P, 2, U], F32, name="skip_rows%d" % u) for u in range(2)]
-        pairs = keep.tile([P, U // GROUP, 2, GROUP], F32, name="pairs", tag="pairs", align_bytes=64)
+        skip_rows = [keep.tile([P, 2, DIRECT], F32, name="skip_rows%d" % u) for u in range(2)]
+        skip_turn = keep.tile([P, PACK, U - DIRECT], F32, name="skip_turn")
+        pairs = keep.tile([P, DIRECT // GROUP, 2, GROUP], F32, name="pairs", align_bytes=64)
+        ident = keep.tile([P, P], F32, name="ident")
         up = [keep.tile([P, U], F32, name="up%d" % t, tag="up%d" % t) for t in range(PACK)]
         w2_codes = keep.tile([P, N], U32, name="w2_codes", align_bytes=64)
         w2_plane = keep.tile([P, N], U8, name="w2_plane", align_bytes=64)
-        ident = keep.tile([P, P], F32, name="ident")
 
         x_by_slot = xT.rearrange("(p j) c -> p j c", j=PACK)
         w1_by_slot = w1.rearrange("(p j) c -> p j c", j=PACK)
@@ -71,12 +68,13 @@ def tile_picked_unet_relu_e_kernel(tc, xT, w1, w2_words, w2_scales, skip, offs, 
         for u in range(2):
             nc.sync.dma_start(out=w1_rows[u][:], in_=w1_by_slot[:, 2 * u : 2 * u + 2, :])
         nc.sync.dma_start(cell_sb[:], cell)
-        for u in (1, 0):
-            nc.sync.dma_start(out=skip_rows[u][:], in_=skip_by_slot[:, 2 * u : 2 * u + 2, :])
+        nc.sync.dma_start(out=skip_rows[0][:], in_=skip_by_slot[:, 0:2, :DIRECT])
         nc.sync.dma_start(out=w2_codes[:].bitcast(I32), in_=w2_words[0].rearrange("p n t -> p (n t)").bitcast(I32))
         nc.vector.memset(w2_plane[:].bitcast(I32), 0)
         for q in range(4):
             nc.sync.dma_start(out=w2_plane[32 * q : 32 * q + 4, :].bitcast(I32), in_=w2_scales[0, 4 * q : 4 * q + 4, :].bitcast(I32))
+        nc.sync.dma_start(out=skip_turn[:], in_=skip_by_slot[:, :, DIRECT:])
+        nc.sync.dma_start(out=skip_rows[1][:], in_=skip_by_slot[:, 2:4, :DIRECT])
 
         for t in range(PACK):
             nc.vector.memset(up[t][:], 0.0)
@@ -90,10 +88,7 @@ def tile_picked_unet_relu_e_kernel(tc, xT, w1, w2_words, w2_scales, skip, offs, 
                                   x_rows[PACK - 1][:].indirect(offs_sb[:, first // LIST_ROWS : (first + HALF) // LIST_ROWS]))
         x_codes = keep.tile([P, S], U32, name="x_codes", align_bytes=64)
         x_plane = keep.tile([P, S], U8, name="x_plane", align_bytes=64)
-        w1_low = keep.tile([P, 2, P, PACK], BF16, name="w1_low", align_bytes=64)
-        w1_first = keep.tile([P, P, PACK], BF16, name="w1_first", align_bytes=64)
-        w1_last = keep.tile([P, P, PACK], BF16, name="w1_last", align_bytes=64)
-        w1_bf = [w1_low[:, 0, :, :], w1_low[:, 1, :, :], w1_first[:], w1_last[:]]
+        w1_pair = [keep.tile([P, 2, P, PACK], BF16, name="w1_pair%d" % h, align_bytes=64) for h in range(2)]
         w1_codes = keep.tile([P, H], U32, name="w1_codes", align_bytes=64)
         w1_plane = keep.tile([P, H], U8, name="w1_plane", align_bytes=64)
         hidden = [keep.tile([P, S], F32, name="hidden%d" % t) for t in range(PACK)]
@@ -102,145 +97,177 @@ def tile_picked_unet_relu_e_kernel(tc, xT, w1, w2_words, w2_scales, skip, offs, 
             nc.vector.quantize_mx(out=x_codes[:, cols].bitcast(FP8X4), scales=x_plane[:, cols],
                                   in_=picked[:, cols, :].rearrange("p s j -> p (s j)"))
 
-        def deal_w1(copy, u, t):
-            copy(w1_bf[t][:, :, 2 * u : 2 * u + 2], w1_rows[u][:].rearrange("p j (m t) -> p m j t", t=PACK)[:, :, :, t])
+        def deal(copy, u, h):
+            copy(w1_pair[h][:, :, :, 2 * u : 2 * u + 2].rearrange("p t m j -> p m t j"),
+                 w1_rows[u][:].rearrange("p j (m t) -> p m t j", t=PACK)[:, :, 2 * h : 2 * h + 2, :])
 
-        def deal_low(copy, u):
-            copy(w1_low[:, :, :, 2 * u : 2 * u + 2].rearrange("p t m j -> p m t j"),
-                 w1_rows[u][:].rearrange("p j (m t) -> p m t j", t=PACK)[:, :, 0:2, :])
-
-        def quantize_w1(t):
-            cols = slice(t * P, (t + 1) * P)
+        def quantize_w1(h):
+            cols = slice(2 * h * P, (2 * h + 2) * P)
             nc.vector.quantize_mx(out=w1_codes[:, cols].bitcast(FP8X4), scales=w1_plane[:, cols],
-                                  in_=w1_bf[t].rearrange("p m j -> p (m j)"))
+                                  in_=w1_pair[h][:].rearrange("p t m j -> p (t m j)"))
 
-        def first_layer(t, cols):
-            acc = psum.tile([P, BANK], F32, name="acc")
-            width = cols.stop - cols.start
+        def bank(b):
+            return psum.tile([P, BANK], F32, name="bank", tag="bank%d" % b)
+
+        def first_layer(t, pieces, b):
+            acc = bank(b)
             mine = slice(t * P, (t + 1) * P)
-            nc.tensor.matmul_mx(out=acc[:, :width], lhsT=w1_codes[:, mine].bitcast(FP8X4), lhsT_scale=w1_plane[:, mine],
-                                rhs=x_codes[:, cols].bitcast(FP8X4), rhs_scale=x_plane[:, cols], start=True, stop=True)
-            nc.scalar.activation(hidden[t][:, cols], acc[:, :width], RELU)
+            for cols in pieces:
+                nc.tensor.matmul_mx(out=acc[:, cols], lhsT=w1_codes[:, mine].bitcast(FP8X4), lhsT_scale=w1_plane[:, mine],
+                                    rhs=x_codes[:, cols].bitcast(FP8X4), rhs_scale=x_plane[:, cols], start=True, stop=True)
+            return acc
 
-        def scatter(t, cols):
-            entries = cell_sb[:, cols.start // LIST_ROWS : cols.stop // LIST_ROWS]
-            nc.vector.tensor_copy(up[t][:].indirect(entries), hidden[t][:, cols])
+        def entries(cols):
+            return cell_sb[:, cols.start // LIST_ROWS : cols.stop // LIST_ROWS]
+
+        def relu_on_scalar(values, acc, cols):
+            nc.scalar.activation(values, acc[:, cols], RELU)
+
+        def relu_on_vector(values, acc, cols):
+            nc.vector.tensor_scalar_max(values, acc[:, cols], 0.0)
+
+        def scatter_on_scalar(t, cols, values):
+            nc.scalar.activation(up[t][:].indirect(entries(cols)), values, COPY)
+
+        def scatter_on_vector(t, cols, values):
+            nc.vector.tensor_copy(up[t][:].indirect(entries(cols)), values)
 
         def by_group(ap):
             return ap.rearrange("p (g v) -> p g v", v=GROUP)
 
-        def slot_halves(t, cols):
-            words = pairs[:, cols.start // GROUP : cols.stop // GROUP, t // 2, :]
-            return words.bitcast(BF16).rearrange("p g (v e) -> p g v e", e=2)[:, :, :, t % 2]
-
-        def fill_words(u):
-            words = pairs[:, :, u, :].bitcast(BF16).rearrange("p g (v e) -> p g v e", e=2)
-            nc.scalar.copy(words, skip_rows[u][:].rearrange("p e (g v) -> p g v e", v=GROUP))
+        def add_skip(engine, t, cols, rows):
+            words = rows[:, :, t // 2, :]
+            halves = words.bitcast(BF16).rearrange("p g (v e) -> p g v e", e=2)[:, :, :, t % 2]
+            engine.tensor_tensor(halves, by_group(up[t][:, cols]), by_group(skip_rows[t // 2][:, t % 2, cols]), ADD)
 
         lead = slice(0, LEAD)
         second = slice(LEAD, HALF)
+        early = slice(0, HALF)
         late = slice(HALF, S)
         rest = slice(LEAD, S)
         whole = slice(0, S)
-        s0, s1, s2, s3 = ORDER
 
-        deal_w1(nc.scalar.copy, 0, s0)
-        deal_low(nc.scalar.copy, 0)
-        deal_w1(nc.scalar.copy, 0, s3)
-        quantize_x(lead)
-        quantize_x(second)
-        deal_w1(nc.vector.tensor_copy, 1, s0)
-        deal_w1(nc.scalar.copy, 1, s3)
-        quantize_w1(s0)
-        first_layer(s0, lead)
+        deal(nc.scalar.copy, 0, 0)
+        deal(nc.scalar.copy, 0, 1)
+        quantize_x(early)
         quantize_x(late)
-        deal_low(nc.vector.tensor_copy, 1)
-        quantize_w1(s1)
-        first_layer(s1, lead)
-        quantize_w1(s2)
-        quantize_w1(s3)
-        for t in (s0, s1):
-            first_layer(t, second)
-            first_layer(t, late)
-        scatter(s0, lead)
-        scatter(s1, lead)
-        scatter(s0, rest)
-        for t in (s2, s3):
-            first_layer(t, whole)
-        nc.gpsimd.tensor_tensor(skip_rows[1][:, 0, :], up[2][:], skip_rows[1][:, 0, :], ADD)
-        scatter(s1, rest)
+        deal(nc.vector.tensor_copy, 1, 0)
+        deal(nc.scalar.copy, 1, 1)
+        quantize_w1(0)
+        acc = first_layer(0, [early], 0)
+        relu_on_scalar(hidden[0][:, early], acc, early)
+        acc = first_layer(1, [lead], 1)
+        relu_on_vector(hidden[1][:, lead], acc, lead)
+        quantize_w1(1)
+        scatter_on_vector(1, lead, hidden[1][:, lead])
+        acc = first_layer(0, [late], 2)
+        relu_on_scalar(hidden[0][:, late], acc, late)
+        for cols in (early, late):
+            scatter_on_scalar(0, cols, hidden[0][:, cols])
+        acc = first_layer(1, [second, late], 3)
+        relu_on_vector(hidden[1][:, rest], acc, rest)
+        scatter_on_vector(1, rest, hidden[1][:, rest])
+        relu_on_scalar(hidden[2][:, early], first_layer(2, [early], 4), early)
+        relu_on_vector(hidden[2][:, late], first_layer(2, [late], 1), late)
+        relu_on_scalar(hidden[3][:], first_layer(3, [whole], 5), whole)
+        for cols in (early, late):
+            scatter_on_vector(2, cols, hidden[2][:, cols])
+        for cols in (early, late):
+            scatter_on_scalar(3, cols, hidden[3][:, cols])
+        sums = [bank(b) for b in (6, 7, 0)]
 
-        def stage_skip(cols, tag, there):
-            width = cols.stop - cols.start
-            for v in range(0, width, P):
-                nc.tensor.transpose(there[:, v : v + P], skip_rows[1][:, 1, cols.start + v : cols.start + v + P], ident[:])
-            turned = keep.tile([P, width], F32, name="turned%d" % cols.start, tag=tag)
-            nc.scalar.copy(turned[:], there[:, :width])
-            back = held.tile([P, BANK], F32, name="staged%d" % cols.start, tag="staged%d" % (cols.start // BANK))
-            for v in range(0, width, P):
-                nc.tensor.transpose(back[:, v : v + P], turned[:, v : v + P], ident[:])
-            return back
+        def turn_in(b, t, rows, start, stop):
+            nc.tensor.matmul(sums[b][:, t * P : (t + 1) * P], rows, ident[:], start=start, stop=stop, is_transpose=True)
 
-        staged = [stage_skip(spans_of(STAGED)[0], "turned", psum.tile([P, BANK], F32, name="acc"))]
+        def turn_up(slots):
+            for t in slots:
+                for b in range(TURNED):
+                    turn_in(b, t, up[t][:, DIRECT + b * P : DIRECT + (b + 1) * P], False, t == PACK - 1)
 
-        fill_words(1)
-        cells = slice(0, U)
-        nc.gpsimd.tensor_tensor(slot_halves(0, cells), by_group(up[0][:]), by_group(skip_rows[0][:, 0, :]), ADD)
-        scatter(s2, whole)
-        nc.gpsimd.tensor_tensor(slot_halves(1, cells), by_group(up[1][:]), by_group(skip_rows[0][:, 1, :]), ADD)
-        staged.append(stage_skip(spans_of(STAGED)[1], "up1", held.tile([P, BANK], F32, name="there", tag="spare")))
-        scatter(s3, whole)
-        for cols in spans_of(ADD_PIECES):
-            bank = 0 if cols.start < STAGED[0] else 1
-            first = cols.start - bank * STAGED[0]
-            nc.vector.tensor_tensor(slot_halves(3, cols), by_group(up[3][:, cols]),
-                                    by_group(staged[bank][:, first : first + cols.stop - cols.start]), ADD)
-        tail = slice(VECTOR_CELLS, U)
-        nc.gpsimd.tensor_tensor(slot_halves(3, tail), by_group(up[3][:, tail]), by_group(skip_rows[1][:, 1, tail]), ADD)
+        for b in range(TURNED):
+            for t in range(PACK):
+                turn_in(b, t, skip_turn[:, t, b * P : (b + 1) * P], t == 0, False)
+        turn_up((0, 1))
+        for cols in spans_of((FRONT, DIRECT - FRONT)):
+            for t in (0, 1):
+                add_skip(nc.gpsimd, t, cols, pairs[:, cols.start // GROUP : cols.stop // GROUP, :, :])
 
         out_by_tile = out.rearrange("(a p) v -> p a v", p=P)
+        spans = spans_of(CHUNKS + (2 * P, P))
+        z = [keep.tile([P, 2 * (cols.stop - cols.start)], F32, name="z%d" % c, tag="z%d" % c, align_bytes=64) for c, cols in enumerate(spans)]
         z_codes = {}
-        z_plane = {}
-        for c in CHUNK_ORDER:
-            cols = spans_of(CHUNKS)[c]
-            width = cols.stop - cols.start
-            z = keep.tile([P, width // GROUP, GROUP, 2], I32, name="z%d" % c, tag="z0" if c in WEAVE_ON_VECTOR else "z%d" % c, align_bytes=64)
-            pair_rows = pairs[:, cols.start // GROUP : cols.stop // GROUP, :, :]
-            if c in WEAVE_ON_VECTOR:
-                nc.vector.tensor_copy(z[:], pair_rows.bitcast(I32).rearrange("p g u v -> p g v u"))
-            else:
-                nc.scalar.copy(z[:].bitcast(U32), pair_rows.bitcast(U32).rearrange("p g u v -> p g v u"))
-            z_codes[c] = keep.tile([P, width], U32, name="z_codes%d" % c, align_bytes=64)
-            z_plane[c] = keep.tile([P, width], U8, name="z_plane%d" % c, align_bytes=64)
-            nc.vector.quantize_mx(out=z_codes[c][:].bitcast(FP8X4), scales=z_plane[c][:],
-                                  in_=z[:].rearrange("p g v u -> p (g v u)").bitcast(BF16))
+        z_plane = [keep.tile([P, cols.stop - cols.start], U8, name="z_plane%d" % c, align_bytes=64) for c, cols in enumerate(spans)]
+        rounded = [keep.tile([P, 2, P, 2], BF16, name="rounded%d" % b, align_bytes=64) for b in range(TURNED)]
+
+        def pair_rows(c):
+            return pairs[:, spans[c].start // GROUP : spans[c].stop // GROUP, :, :]
+
+        def add_high(t, c):
+            add_skip(nc.vector, t, spans[c], pair_rows(c))
+
+        def weave(c):
+            nc.vector.tensor_copy(z[c][:].bitcast(I32).rearrange("p (g v u) -> p g v u", v=GROUP, u=2), pair_rows(c).bitcast(I32).rearrange("p g u v -> p g v u"))
+
+        def round_sums(b):
+            nc.scalar.copy(rounded[b][:], sums[b][:].rearrange("c (u e p) -> c u p e", u=2, e=2))
+
+        def turn_back(b, into):
+            back = bank(into)
+            words = rounded[b][:].rearrange("c u p e -> c (u p e)").bitcast(F32)
+            for u in range(2):
+                nc.tensor.transpose(back[:, u * P : (u + 1) * P], words[:, u * P : (u + 1) * P], ident[:])
+            mine = z[len(CHUNKS) + b // 2][:, (b % 2) * 2 * P : (b % 2 + 1) * 2 * P]
+            nc.scalar.copy(mine.rearrange("p (v u) -> p v u", u=2), back[:, : 2 * P].rearrange("p (u v) -> p v u", u=2))
+
+        def quantize_z(c):
+            tag = "z%d" % (c - 2) if c >= len(CHUNKS) else "z_codes%d" % c
+            z_codes[c] = keep.tile([P, spans[c].stop - spans[c].start], U32, name="z_codes%d" % c, tag=tag, align_bytes=64)
+            nc.vector.quantize_mx(out=z_codes[c][:].bitcast(FP8X4), scales=z_plane[c][:], in_=z[c][:].bitcast(BF16))
 
         def second_layer(acc, a, c):
             nc.tensor.matmul_mx(out=acc, lhsT=w2_codes[:, a * P : (a + 1) * P].bitcast(FP8X4),
                                 lhsT_scale=w2_plane[:, a * P : (a + 1) * P], rhs=z_codes[c][:].bitcast(FP8X4), rhs_scale=z_plane[c][:],
                                 start=True, stop=True)
 
-        for c in CHUNK_ORDER:
-            cols = spans_of(CHUNKS)[c]
+        def finish(c, b, copy):
+            cols = spans[c]
             width = cols.stop - cols.start
-            if c in SPLIT_EXIT:
-                for a in range(N // P):
-                    if c == CHUNK_ORDER[-1]:
-                        acc = held.tile([P, BANK], F32, name="last%d" % a, tag="staged%d" % a)
-                    else:
-                        acc = psum.tile([P, BANK], F32, name="acc")
-                    second_layer(acc[:, :width], a, c)
-                    if a == 0:
-                        result = keep.tile([P, width], F32, name="result%d_0" % c)
-                        nc.scalar.copy(result[:], acc[:, :width])
-                    else:
-                        result = keep.tile([P, width], F32, name="result%d_1" % c, tag="z3" if c == SPLIT_EXIT[0] else "result%d_1" % c, align_bytes=64)
-                        nc.vector.tensor_copy(result[:], acc[:, :width])
-                    nc.sync.dma_start(out=out_by_tile[:, a, cols], in_=result[:])
-            else:
-                acc = held.tile([P, BANK], F32, name="first", tag="spare") if c == 0 else psum.tile([P, BANK], F32, name="acc")
-                for a in range(N // P):
-                    second_layer(acc[:, a * width : (a + 1) * width], a, c)
-                result = keep.tile([P, N // P, width], F32, name="result%d" % c, tag="pairs" if c == 0 else "result%d" % c, align_bytes=64)
-                nc.scalar.copy(result[:].rearrange("p a v -> p (a v)"), acc[:, : 2 * width])
-                nc.sync.dma_start(out=out_by_tile[:, :, cols], in_=result[:])
+            acc = bank(b)
+            for a in range(N // P):
+                second_layer(acc[:, a * width : (a + 1) * width], a, c)
+            result = keep.tile([P, N // P, width], F32, name="result%d" % c)
+            copy(result[:].rearrange("p a v -> p (a v)"), acc[:, : 2 * width])
+            nc.sync.dma_start(out=out_by_tile[:, :, cols], in_=result[:])
+
+        def finish_split(c, banks):
+            cols = spans[c]
+            width = cols.stop - cols.start
+            for a, copy in enumerate((nc.scalar.copy, nc.vector.tensor_copy)):
+                acc = bank(banks[a])
+                second_layer(acc[:, :width], a, c)
+                result = keep.tile([P, width], F32, name="result%d_%d" % (c, a))
+                copy(result[:], acc[:, :width])
+                nc.sync.dma_start(out=out_by_tile[:, a, cols], in_=result[:])
+
+        turn_up((2, 3))
+        for t, c in ((2, 0), (2, 1), (3, 0), (3, 1)):
+            add_high(t, c)
+        for b in range(TURNED):
+            round_sums(b)
+        weave(0)
+        add_high(2, 2)
+        quantize_z(0)
+        weave(1)
+        add_high(3, 2)
+        quantize_z(1)
+        weave(2)
+        for b in range(TURNED):
+            turn_back(b, (1, 3, 5)[b])
+        finish(0, 2, nc.vector.tensor_copy)
+        finish(1, 4, nc.vector.tensor_copy)
+        quantize_z(3)
+        quantize_z(2)
+        quantize_z(4)
+        finish(3, 6, nc.scalar.copy)
+        finish_split(2, (7, 0))
+        finish_split(4, (1, 2))

@@ -1,7 +1,6 @@
 from contextlib import ExitStack
 
 import concourse.mybir as mybir
-from concourse.masks import make_identity
 
 K, T, S, H, N, U = 512, 2048, 512, 512, 256, 1024
 FLOPS = 2 * K * H * S + 2 * H * N * U
@@ -25,9 +24,8 @@ HALF = S // 2
 LEAD = 128
 GROUP = 128
 FRONT = 384
-DIRECT = 640
-CHUNKS = (128, 256, 256)
-TURNED = (U - DIRECT) // P
+WEAVE_ON_VECTOR = (4,)
+CHUNKS = (128, 256, 256, 256, 128)
 
 
 def spans_of(widths):
@@ -49,10 +47,10 @@ def tile_picked_unet_relu_e_kernel(tc, xT, w1, w2_words, w2_scales, skip, offs, 
         cell_sb = keep.tile([P, S // LIST_ROWS], U16, name="cell_sb")
         x_rows = [keep.tile([P, T], F32, name="x_rows%d" % j) for j in range(PACK)]
         w1_rows = [keep.tile([P, 2, H], F32, name="w1_rows%d" % u) for u in range(2)]
-        skip_rows = [keep.tile([P, 2, DIRECT], F32, name="skip_rows%d" % u) for u in range(2)]
-        skip_turn = keep.tile([P, PACK, U - DIRECT], F32, name="skip_turn")
-        pairs = keep.tile([P, DIRECT // GROUP, 2, GROUP], F32, name="pairs", align_bytes=64)
-        ident = keep.tile([P, P], F32, name="ident")
+        skip_rows = [keep.tile([P, 2, U], F32, name="skip_rows%d" % u) for u in range(2)]
+        parts = spans_of((FRONT, U - FRONT))
+        pairs = [keep.tile([P, (cols.stop - cols.start) // GROUP, 2, GROUP], F32, name="pairs%d" % g, tag="pairs%d" % g, align_bytes=64)
+                 for g, cols in enumerate(parts)]
         up = [keep.tile([P, U], F32, name="up%d" % t, tag="up%d" % t) for t in range(PACK)]
         w2_codes = keep.tile([P, N], U32, name="w2_codes", align_bytes=64)
         w2_plane = keep.tile([P, N], U8, name="w2_plane", align_bytes=64)
@@ -68,17 +66,15 @@ def tile_picked_unet_relu_e_kernel(tc, xT, w1, w2_words, w2_scales, skip, offs, 
         for u in range(2):
             nc.sync.dma_start(out=w1_rows[u][:], in_=w1_by_slot[:, 2 * u : 2 * u + 2, :])
         nc.sync.dma_start(cell_sb[:], cell)
-        nc.sync.dma_start(out=skip_rows[0][:], in_=skip_by_slot[:, 0:2, :DIRECT])
+        nc.sync.dma_start(out=skip_rows[0][:], in_=skip_by_slot[:, 0:2, :])
         nc.sync.dma_start(out=w2_codes[:].bitcast(I32), in_=w2_words[0].rearrange("p n t -> p (n t)").bitcast(I32))
         nc.vector.memset(w2_plane[:].bitcast(I32), 0)
         for q in range(4):
             nc.sync.dma_start(out=w2_plane[32 * q : 32 * q + 4, :].bitcast(I32), in_=w2_scales[0, 4 * q : 4 * q + 4, :].bitcast(I32))
-        nc.sync.dma_start(out=skip_turn[:], in_=skip_by_slot[:, :, DIRECT:])
-        nc.sync.dma_start(out=skip_rows[1][:], in_=skip_by_slot[:, 2:4, :DIRECT])
+        nc.sync.dma_start(out=skip_rows[1][:], in_=skip_by_slot[:, 2:4, :])
 
         for t in range(PACK):
             nc.vector.memset(up[t][:], 0.0)
-        make_identity(nc, ident[:])
 
         picked = keep.tile([P, S, PACK], BF16, name="picked", align_bytes=64)
         for j in range(PACK - 1):
@@ -91,7 +87,7 @@ def tile_picked_unet_relu_e_kernel(tc, xT, w1, w2_words, w2_scales, skip, offs, 
         w1_pair = [keep.tile([P, 2, P, PACK], BF16, name="w1_pair%d" % h, align_bytes=64) for h in range(2)]
         w1_codes = keep.tile([P, H], U32, name="w1_codes", align_bytes=64)
         w1_plane = keep.tile([P, H], U8, name="w1_plane", align_bytes=64)
-        hidden = [keep.tile([P, S], F32, name="hidden%d" % t) for t in range(PACK)]
+        hidden = [keep.tile([P, S], F32, name="hidden%d" % t, tag="hidden%d" % t) for t in range(PACK)]
 
         def quantize_x(cols):
             nc.vector.quantize_mx(out=x_codes[:, cols].bitcast(FP8X4), scales=x_plane[:, cols],
@@ -135,8 +131,12 @@ def tile_picked_unet_relu_e_kernel(tc, xT, w1, w2_words, w2_scales, skip, offs, 
         def by_group(ap):
             return ap.rearrange("p (g v) -> p g v", v=GROUP)
 
-        def add_skip(engine, t, cols, rows):
-            words = rows[:, :, t // 2, :]
+        def pair_rows(cols):
+            g = 0 if cols.stop <= FRONT else 1
+            return pairs[g][:, (cols.start - parts[g].start) // GROUP : (cols.stop - parts[g].start) // GROUP, :, :]
+
+        def add_skip(engine, t, cols):
+            words = pair_rows(cols)[:, :, t // 2, :]
             halves = words.bitcast(BF16).rearrange("p g (v e) -> p g v e", e=2)[:, :, :, t % 2]
             engine.tensor_tensor(halves, by_group(up[t][:, cols]), by_group(skip_rows[t // 2][:, t % 2, cols]), ADD)
 
@@ -174,54 +174,22 @@ def tile_picked_unet_relu_e_kernel(tc, xT, w1, w2_words, w2_scales, skip, offs, 
             scatter_on_vector(2, cols, hidden[2][:, cols])
         for cols in (early, late):
             scatter_on_scalar(3, cols, hidden[3][:, cols])
-        sums = [bank(b) for b in (6, 7, 0)]
-
-        def turn_in(b, t, rows, start, stop):
-            nc.tensor.matmul(sums[b][:, t * P : (t + 1) * P], rows, ident[:], start=start, stop=stop, is_transpose=True)
-
-        def turn_up(slots):
-            for t in slots:
-                for b in range(TURNED):
-                    turn_in(b, t, up[t][:, DIRECT + b * P : DIRECT + (b + 1) * P], False, t == PACK - 1)
-
-        for b in range(TURNED):
-            for t in range(PACK):
-                turn_in(b, t, skip_turn[:, t, b * P : (b + 1) * P], t == 0, False)
-        turn_up((0, 1))
-        for cols in spans_of((FRONT, DIRECT - FRONT)):
+        for cols in parts:
             for t in (0, 1):
-                add_skip(nc.gpsimd, t, cols, pairs[:, cols.start // GROUP : cols.stop // GROUP, :, :])
+                add_skip(nc.gpsimd, t, cols)
 
         out_by_tile = out.rearrange("(a p) v -> p a v", p=P)
-        spans = spans_of(CHUNKS + (2 * P, P))
-        z = [keep.tile([P, 2 * (cols.stop - cols.start)], F32, name="z%d" % c, tag="z%d" % c, align_bytes=64) for c, cols in enumerate(spans)]
-        z_codes = {}
-        z_plane = [keep.tile([P, cols.stop - cols.start], U8, name="z_plane%d" % c, align_bytes=64) for c, cols in enumerate(spans)]
-        rounded = [keep.tile([P, 2, P, 2], BF16, name="rounded%d" % b, align_bytes=64) for b in range(TURNED)]
-
-        def pair_rows(c):
-            return pairs[:, spans[c].start // GROUP : spans[c].stop // GROUP, :, :]
-
-        def add_high(t, c):
-            add_skip(nc.vector, t, spans[c], pair_rows(c))
+        spans = spans_of(CHUNKS)
+        z = [keep.tile([P, 2 * width], F32, name="z%d" % c, align_bytes=64) for c, width in enumerate(CHUNKS)]
+        z_codes = [keep.tile([P, width], U32, name="z_codes%d" % c, align_bytes=64) for c, width in enumerate(CHUNKS)]
+        z_plane = [keep.tile([P, width], U8, name="z_plane%d" % c, align_bytes=64) for c, width in enumerate(CHUNKS)]
 
         def weave(c):
-            nc.vector.tensor_copy(z[c][:].bitcast(I32).rearrange("p (g v u) -> p g v u", v=GROUP, u=2), pair_rows(c).bitcast(I32).rearrange("p g u v -> p g v u"))
-
-        def round_sums(b):
-            nc.scalar.copy(rounded[b][:], sums[b][:].rearrange("c (u e p) -> c u p e", u=2, e=2))
-
-        def turn_back(b, into):
-            back = bank(into)
-            words = rounded[b][:].rearrange("c u p e -> c (u p e)").bitcast(F32)
-            for u in range(2):
-                nc.tensor.transpose(back[:, u * P : (u + 1) * P], words[:, u * P : (u + 1) * P], ident[:])
-            mine = z[len(CHUNKS) + b // 2][:, (b % 2) * 2 * P : (b % 2 + 1) * 2 * P]
-            nc.scalar.copy(mine.rearrange("p (v u) -> p v u", u=2), back[:, : 2 * P].rearrange("p (u v) -> p v u", u=2))
+            rows = pair_rows(spans[c])
+            copy, words = (nc.vector.tensor_copy, I32) if c in WEAVE_ON_VECTOR else (nc.scalar.copy, U32)
+            copy(z[c][:].bitcast(words).rearrange("p (g v u) -> p g v u", v=GROUP, u=2), rows.bitcast(words).rearrange("p g u v -> p g v u"))
 
         def quantize_z(c):
-            tag = "z%d" % (c - 2) if c >= len(CHUNKS) else "z_codes%d" % c
-            z_codes[c] = keep.tile([P, spans[c].stop - spans[c].start], U32, name="z_codes%d" % c, tag=tag, align_bytes=64)
             nc.vector.quantize_mx(out=z_codes[c][:].bitcast(FP8X4), scales=z_plane[c][:], in_=z[c][:].bitcast(BF16))
 
         def second_layer(acc, a, c):
@@ -235,7 +203,7 @@ def tile_picked_unet_relu_e_kernel(tc, xT, w1, w2_words, w2_scales, skip, offs, 
             acc = bank(b)
             for a in range(N // P):
                 second_layer(acc[:, a * width : (a + 1) * width], a, c)
-            result = keep.tile([P, N // P, width], F32, name="result%d" % c)
+            result = keep.tile([P, N // P, width], F32, name="result%d" % c, tag="pairs1" if c == 1 else "result%d" % c, align_bytes=64)
             copy(result[:].rearrange("p a v -> p (a v)"), acc[:, : 2 * width])
             nc.sync.dma_start(out=out_by_tile[:, :, cols], in_=result[:])
 
@@ -249,25 +217,24 @@ def tile_picked_unet_relu_e_kernel(tc, xT, w1, w2_words, w2_scales, skip, offs, 
                 copy(result[:], acc[:, :width])
                 nc.sync.dma_start(out=out_by_tile[:, a, cols], in_=result[:])
 
-        turn_up((2, 3))
-        for t, c in ((2, 0), (2, 1), (3, 0), (3, 1)):
-            add_high(t, c)
-        for b in range(TURNED):
-            round_sums(b)
-        weave(0)
-        add_high(2, 2)
+        def add_high(c):
+            cols = spans[c]
+            for t in (2, 3):
+                add_skip(nc.vector, t, cols)
+            weave(c)
+
+        add_high(0)
+        add_high(1)
         quantize_z(0)
-        weave(1)
-        add_high(3, 2)
+        add_high(2)
         quantize_z(1)
-        weave(2)
-        for b in range(TURNED):
-            turn_back(b, (1, 3, 5)[b])
-        finish(0, 2, nc.vector.tensor_copy)
-        finish(1, 4, nc.vector.tensor_copy)
-        quantize_z(3)
+        finish(0, 0, nc.scalar.copy)
+        add_high(3)
         quantize_z(2)
+        add_high(4)
+        finish(1, 1, nc.scalar.copy)
+        quantize_z(3)
         quantize_z(4)
-        finish(3, 6, nc.scalar.copy)
-        finish_split(2, (7, 0))
-        finish_split(4, (1, 2))
+        finish(2, 2, nc.scalar.copy)
+        finish_split(3, (3, 4))
+        finish_split(4, (6, 7))

@@ -23,9 +23,9 @@ LIST_ROWS = 16
 HALF = S // 2
 LEAD = 128
 GROUP = 128
-FRONT = 384
+GPSIMD_CELLS = 768
+CHUNKS = (128, 256, 384, 128, 128)
 WEAVE_ON_VECTOR = (4,)
-CHUNKS = (128, 256, 256, 256, 128)
 
 
 def spans_of(widths):
@@ -48,9 +48,7 @@ def tile_picked_unet_relu_e_kernel(tc, xT, w1, w2_words, w2_scales, skip, offs, 
         x_rows = [keep.tile([P, T], F32, name="x_rows%d" % j) for j in range(PACK)]
         w1_rows = [keep.tile([P, 2, H], F32, name="w1_rows%d" % u) for u in range(2)]
         skip_rows = [keep.tile([P, 2, U], F32, name="skip_rows%d" % u) for u in range(2)]
-        parts = spans_of((FRONT, U - FRONT))
-        pairs = [keep.tile([P, (cols.stop - cols.start) // GROUP, 2, GROUP], F32, name="pairs%d" % g, tag="pairs%d" % g, align_bytes=64)
-                 for g, cols in enumerate(parts)]
+        pairs = keep.tile([P, GPSIMD_CELLS // GROUP, 2, GROUP], F32, name="pairs", align_bytes=64)
         up = [keep.tile([P, U], F32, name="up%d" % t, tag="up%d" % t) for t in range(PACK)]
         w2_codes = keep.tile([P, N], U32, name="w2_codes", align_bytes=64)
         w2_plane = keep.tile([P, N], U8, name="w2_plane", align_bytes=64)
@@ -87,7 +85,7 @@ def tile_picked_unet_relu_e_kernel(tc, xT, w1, w2_words, w2_scales, skip, offs, 
         w1_pair = [keep.tile([P, 2, P, PACK], BF16, name="w1_pair%d" % h, align_bytes=64) for h in range(2)]
         w1_codes = keep.tile([P, H], U32, name="w1_codes", align_bytes=64)
         w1_plane = keep.tile([P, H], U8, name="w1_plane", align_bytes=64)
-        hidden = [keep.tile([P, S], F32, name="hidden%d" % t, tag="hidden%d" % t) for t in range(PACK)]
+        hidden = [keep.tile([P, S], F32, name="hidden%d" % t, tag="hidden%d" % t, align_bytes=64) for t in range(PACK)]
 
         def quantize_x(cols):
             nc.vector.quantize_mx(out=x_codes[:, cols].bitcast(FP8X4), scales=x_plane[:, cols],
@@ -131,9 +129,12 @@ def tile_picked_unet_relu_e_kernel(tc, xT, w1, w2_words, w2_scales, skip, offs, 
         def by_group(ap):
             return ap.rearrange("p (g v) -> p g v", v=GROUP)
 
+        late_pairs = {}
+
         def pair_rows(cols):
-            g = 0 if cols.stop <= FRONT else 1
-            return pairs[g][:, (cols.start - parts[g].start) // GROUP : (cols.stop - parts[g].start) // GROUP, :, :]
+            if cols.stop <= GPSIMD_CELLS:
+                return pairs[:, cols.start // GROUP : cols.stop // GROUP, :, :]
+            return late_pairs[cols.start][:]
 
         def add_skip(engine, t, cols):
             words = pair_rows(cols)[:, :, t // 2, :]
@@ -174,13 +175,12 @@ def tile_picked_unet_relu_e_kernel(tc, xT, w1, w2_words, w2_scales, skip, offs, 
             scatter_on_vector(2, cols, hidden[2][:, cols])
         for cols in (early, late):
             scatter_on_scalar(3, cols, hidden[3][:, cols])
-        for cols in parts:
-            for t in (0, 1):
-                add_skip(nc.gpsimd, t, cols)
+        for t in (0, 1):
+            add_skip(nc.gpsimd, t, slice(0, GPSIMD_CELLS))
 
         out_by_tile = out.rearrange("(a p) v -> p a v", p=P)
         spans = spans_of(CHUNKS)
-        z = [keep.tile([P, 2 * width], F32, name="z%d" % c, align_bytes=64) for c, width in enumerate(CHUNKS)]
+        z = [keep.tile([P, 2 * width], F32, name="z%d" % c, tag="z%d" % c, align_bytes=64) for c, width in enumerate(CHUNKS)]
         z_codes = [keep.tile([P, width], U32, name="z_codes%d" % c, align_bytes=64) for c, width in enumerate(CHUNKS)]
         z_plane = [keep.tile([P, width], U8, name="z_plane%d" % c, align_bytes=64) for c, width in enumerate(CHUNKS)]
 
@@ -193,9 +193,11 @@ def tile_picked_unet_relu_e_kernel(tc, xT, w1, w2_words, w2_scales, skip, offs, 
             nc.vector.quantize_mx(out=z_codes[c][:].bitcast(FP8X4), scales=z_plane[c][:], in_=z[c][:].bitcast(BF16))
 
         def second_layer(acc, a, c):
-            nc.tensor.matmul_mx(out=acc, lhsT=w2_codes[:, a * P : (a + 1) * P].bitcast(FP8X4),
-                                lhsT_scale=w2_plane[:, a * P : (a + 1) * P], rhs=z_codes[c][:].bitcast(FP8X4), rhs_scale=z_plane[c][:],
-                                start=True, stop=True)
+            for first in range(0, CHUNKS[c], 2 * P):
+                cols = slice(first, min(first + 2 * P, CHUNKS[c]))
+                nc.tensor.matmul_mx(out=acc[:, cols], lhsT=w2_codes[:, a * P : (a + 1) * P].bitcast(FP8X4),
+                                    lhsT_scale=w2_plane[:, a * P : (a + 1) * P], rhs=z_codes[c][:, cols].bitcast(FP8X4),
+                                    rhs_scale=z_plane[c][:, cols], start=True, stop=True)
 
         def finish(c, b, copy):
             cols = spans[c]
@@ -203,14 +205,14 @@ def tile_picked_unet_relu_e_kernel(tc, xT, w1, w2_words, w2_scales, skip, offs, 
             acc = bank(b)
             for a in range(N // P):
                 second_layer(acc[:, a * width : (a + 1) * width], a, c)
-            result = keep.tile([P, N // P, width], F32, name="result%d" % c, tag="pairs1" if c == 1 else "result%d" % c, align_bytes=64)
+            result = keep.tile([P, N // P, width], F32, name="result%d" % c)
             copy(result[:].rearrange("p a v -> p (a v)"), acc[:, : 2 * width])
             nc.sync.dma_start(out=out_by_tile[:, :, cols], in_=result[:])
 
-        def finish_split(c, banks):
+        def finish_split(c, banks, copies):
             cols = spans[c]
             width = cols.stop - cols.start
-            for a, copy in enumerate((nc.scalar.copy, nc.vector.tensor_copy)):
+            for a, copy in enumerate(copies):
                 acc = bank(banks[a])
                 second_layer(acc[:, :width], a, c)
                 result = keep.tile([P, width], F32, name="result%d_%d" % (c, a))
@@ -219,22 +221,23 @@ def tile_picked_unet_relu_e_kernel(tc, xT, w1, w2_words, w2_scales, skip, offs, 
 
         def add_high(c):
             cols = spans[c]
-            for t in (2, 3):
+            if cols.start >= GPSIMD_CELLS:
+                late_pairs[cols.start] = keep.tile([P, 1, 2, GROUP], F32, name="late_pairs%d" % c, tag="z%d" % (c - 3), align_bytes=64)
+            for t in range(2 if cols.stop <= GPSIMD_CELLS else 0, PACK):
                 add_skip(nc.vector, t, cols)
             weave(c)
 
-        add_high(0)
-        add_high(1)
+        for c in range(3):
+            add_high(c)
         quantize_z(0)
-        add_high(2)
         quantize_z(1)
         finish(0, 0, nc.scalar.copy)
         add_high(3)
+        finish(1, 1, nc.scalar.copy)
         quantize_z(2)
         add_high(4)
-        finish(1, 1, nc.scalar.copy)
+        finish_split(2, (2, 3), (nc.scalar.copy, nc.scalar.copy))
         quantize_z(3)
         quantize_z(4)
-        finish(2, 2, nc.scalar.copy)
-        finish_split(3, (3, 4))
-        finish_split(4, (6, 7))
+        finish(3, 4, nc.vector.tensor_copy)
+        finish_split(4, (6, 7), (nc.scalar.copy, nc.vector.tensor_copy))

@@ -25,7 +25,6 @@ LEAD = 128
 GROUP = 128
 GPSIMD_CELLS = 768
 CHUNKS = (128, 256, 384, 128, 128)
-WEAVE_ON_VECTOR = (4,)
 
 
 def spans_of(widths):
@@ -129,12 +128,8 @@ def tile_picked_unet_relu_e_kernel(tc, xT, w1, w2_words, w2_scales, skip, offs, 
         def by_group(ap):
             return ap.rearrange("p (g v) -> p g v", v=GROUP)
 
-        late_pairs = {}
-
         def pair_rows(cols):
-            if cols.stop <= GPSIMD_CELLS:
-                return pairs[:, cols.start // GROUP : cols.stop // GROUP, :, :]
-            return late_pairs[cols.start][:]
+            return pairs[:, cols.start // GROUP : cols.stop // GROUP, :, :]
 
         def add_skip(engine, t, cols):
             words = pair_rows(cols)[:, :, t // 2, :]
@@ -186,8 +181,7 @@ def tile_picked_unet_relu_e_kernel(tc, xT, w1, w2_words, w2_scales, skip, offs, 
 
         def weave(c):
             rows = pair_rows(spans[c])
-            copy, words = (nc.vector.tensor_copy, I32) if c in WEAVE_ON_VECTOR else (nc.scalar.copy, U32)
-            copy(z[c][:].bitcast(words).rearrange("p (g v u) -> p g v u", v=GROUP, u=2), rows.bitcast(words).rearrange("p g u v -> p g v u"))
+            nc.scalar.copy(z[c][:].bitcast(U32).rearrange("p (g v u) -> p g v u", v=GROUP, u=2), rows.bitcast(U32).rearrange("p g u v -> p g v u"))
 
         def quantize_z(c):
             nc.vector.quantize_mx(out=z_codes[c][:].bitcast(FP8X4), scales=z_plane[c][:], in_=z[c][:].bitcast(BF16))
@@ -219,23 +213,24 @@ def tile_picked_unet_relu_e_kernel(tc, xT, w1, w2_words, w2_scales, skip, offs, 
                 copy(result[:], acc[:, :width])
                 nc.sync.dma_start(out=out_by_tile[:, a, cols], in_=result[:])
 
-        def add_high(c):
+        def add_all(c, copy):
             cols = spans[c]
-            if cols.start >= GPSIMD_CELLS:
-                late_pairs[cols.start] = keep.tile([P, 1, 2, GROUP], F32, name="late_pairs%d" % c, tag="z%d" % (c - 3), align_bytes=64)
-            for t in range(2 if cols.stop <= GPSIMD_CELLS else 0, PACK):
-                add_skip(nc.vector, t, cols)
-            weave(c)
+            sums = keep.tile([P, PACK, CHUNKS[c]], F32, name="sums%d" % c, tag="z%d" % (c - 3), align_bytes=64)
+            for t in range(PACK):
+                nc.vector.tensor_tensor(sums[:, t, :], up[t][:, cols], skip_rows[t // 2][:, t % 2, cols], ADD)
+            copy(z[c][:].bitcast(BF16).rearrange("p (g v t) -> p g t v", v=4, t=PACK), sums[:].rearrange("p t (g v) -> p g t v", v=4))
 
         for c in range(3):
-            add_high(c)
+            for t in (2, 3):
+                add_skip(nc.vector, t, spans[c])
+            weave(c)
         quantize_z(0)
         quantize_z(1)
         finish(0, 0, nc.scalar.copy)
-        add_high(3)
+        add_all(3, nc.scalar.copy)
         finish(1, 1, nc.scalar.copy)
         quantize_z(2)
-        add_high(4)
+        add_all(4, nc.vector.tensor_copy)
         finish_split(2, (2, 3), (nc.scalar.copy, nc.scalar.copy))
         quantize_z(3)
         quantize_z(4)

@@ -220,10 +220,12 @@ def tile_picked_unet_relu_e_kernel(tc, xT, w1, w2_words, w2_scales, skip, offs, 
                 nc.vector.tensor_tensor(sums[:, t, :], up[t][:, cols], skip_rows[t // 2][:, t % 2, cols], ADD)
             copy(z[c][:].bitcast(BF16).rearrange("p (g v t) -> p g t v", v=4, t=PACK), sums[:].rearrange("p t (g v) -> p g t v", v=4))
 
-        for c in range(3):
+        for group in ((0, 1), (2,)):
             for t in (2, 3):
-                add_skip(nc.vector, t, spans[c])
-            weave(c)
+                for c in group:
+                    add_skip(nc.vector, t, spans[c])
+            for c in group:
+                weave(c)
         quantize_z(0)
         quantize_z(1)
         finish(0, 0, nc.scalar.copy)

@@ -24,6 +24,7 @@ HALF = S // 2
 LEAD = 128
 GROUP = 128
 GPSIMD_CELLS = 768
+FRONT = 384
 CHUNKS = (128, 256, 384, 128, 128)
 
 
@@ -63,11 +64,11 @@ def tile_picked_unet_relu_e_kernel(tc, xT, w1, w2_words, w2_scales, skip, offs, 
         for u in range(2):
             nc.sync.dma_start(out=w1_rows[u][:], in_=w1_by_slot[:, 2 * u : 2 * u + 2, :])
         nc.sync.dma_start(cell_sb[:], cell)
-        nc.sync.dma_start(out=skip_rows[0][:], in_=skip_by_slot[:, 0:2, :])
         nc.sync.dma_start(out=w2_codes[:].bitcast(I32), in_=w2_words[0].rearrange("p n t -> p (n t)").bitcast(I32))
         nc.vector.memset(w2_plane[:].bitcast(I32), 0)
         for q in range(4):
             nc.sync.dma_start(out=w2_plane[32 * q : 32 * q + 4, :].bitcast(I32), in_=w2_scales[0, 4 * q : 4 * q + 4, :].bitcast(I32))
+        nc.sync.dma_start(out=skip_rows[0][:], in_=skip_by_slot[:, 0:2, :])
         nc.sync.dma_start(out=skip_rows[1][:], in_=skip_by_slot[:, 2:4, :])
 
         for t in range(PACK):
@@ -150,24 +151,18 @@ def tile_picked_unet_relu_e_kernel(tc, xT, w1, w2_words, w2_scales, skip, offs, 
         deal(nc.vector.tensor_copy, 1, 0)
         deal(nc.scalar.copy, 1, 1)
         quantize_w1(0)
-        acc = first_layer(0, [early], 0)
-        relu_on_scalar(hidden[0][:, early], acc, early)
-        acc = first_layer(1, [lead], 1)
-        relu_on_vector(hidden[1][:, lead], acc, lead)
+        relu_on_vector(hidden[0][:, lead], first_layer(0, [lead], 0), lead)
         quantize_w1(1)
-        scatter_on_vector(1, lead, hidden[1][:, lead])
-        acc = first_layer(0, [late], 2)
-        relu_on_scalar(hidden[0][:, late], acc, late)
+        scatter_on_vector(0, lead, hidden[0][:, lead])
+        relu_on_scalar(hidden[1][:, early], first_layer(1, [early], 1), early)
+        relu_on_scalar(hidden[0][:, rest], first_layer(0, [second, late], 2), rest)
+        relu_on_scalar(hidden[1][:, late], first_layer(1, [late], 3), late)
+        scatter_on_scalar(0, rest, hidden[0][:, rest])
         for cols in (early, late):
-            scatter_on_scalar(0, cols, hidden[0][:, cols])
-        acc = first_layer(1, [second, late], 3)
-        relu_on_vector(hidden[1][:, rest], acc, rest)
-        scatter_on_vector(1, rest, hidden[1][:, rest])
-        relu_on_scalar(hidden[2][:, early], first_layer(2, [early], 4), early)
-        relu_on_vector(hidden[2][:, late], first_layer(2, [late], 1), late)
-        relu_on_scalar(hidden[3][:], first_layer(3, [whole], 5), whole)
-        for cols in (early, late):
-            scatter_on_vector(2, cols, hidden[2][:, cols])
+            scatter_on_vector(1, cols, hidden[1][:, cols])
+        for t in (2, 3):
+            relu_on_scalar(hidden[t][:], first_layer(t, [whole], 2 + t), whole)
+        scatter_on_vector(2, whole, hidden[2][:])
         for cols in (early, late):
             scatter_on_scalar(3, cols, hidden[3][:, cols])
         for t in (0, 1):
@@ -220,12 +215,13 @@ def tile_picked_unet_relu_e_kernel(tc, xT, w1, w2_words, w2_scales, skip, offs, 
                 nc.vector.tensor_tensor(sums[:, t, :], up[t][:, cols], skip_rows[t // 2][:, t % 2, cols], ADD)
             copy(z[c][:].bitcast(BF16).rearrange("p (g v t) -> p g t v", v=4, t=PACK), sums[:].rearrange("p t (g v) -> p g t v", v=4))
 
-        for group in ((0, 1), (2,)):
-            for t in (2, 3):
-                for c in group:
-                    add_skip(nc.vector, t, spans[c])
-            for c in group:
-                weave(c)
+        add_skip(nc.vector, 2, slice(0, FRONT))
+        for c in range(2):
+            add_skip(nc.vector, 3, spans[c])
+            weave(c)
+        for t in (2, 3):
+            add_skip(nc.vector, t, spans[2])
+        weave(2)
         quantize_z(0)
         quantize_z(1)
         finish(0, 0, nc.scalar.copy)

@@ -21,11 +21,11 @@ PACK = 4
 BANK = 512
 LIST_ROWS = 16
 HALF = S // 2
-LEAD = 128
 GROUP = 128
-GPSIMD_CELLS = 768
-FRONT = 384
-CHUNKS = (128, 256, 384, 128, 128)
+RUN = 8
+OWN = 256
+LEAD = 128
+CHUNKS = (128, 128, 128, 256, 384)
 
 
 def spans_of(widths):
@@ -47,15 +47,20 @@ def tile_picked_unet_relu_e_kernel(tc, xT, w1, w2_words, w2_scales, skip, offs, 
         cell_sb = keep.tile([P, S // LIST_ROWS], U16, name="cell_sb")
         x_rows = [keep.tile([P, T], F32, name="x_rows%d" % j) for j in range(PACK)]
         w1_rows = [keep.tile([P, 2, H], F32, name="w1_rows%d" % u) for u in range(2)]
-        skip_rows = [keep.tile([P, 2, U], F32, name="skip_rows%d" % u) for u in range(2)]
-        pairs = keep.tile([P, GPSIMD_CELLS // GROUP, 2, GROUP], F32, name="pairs", align_bytes=64)
-        up = [keep.tile([P, U], F32, name="up%d" % t, tag="up%d" % t) for t in range(PACK)]
+        skip23 = keep.tile([P, 2, U], F32, name="skip23")
+        skip0 = keep.tile([P, U - OWN], F32, name="skip0")
+        skip01 = keep.tile([P, 2, OWN], F32, name="skip01")
+        pairs = keep.tile([P, (U - OWN) // GROUP, 2, GROUP], F32, name="pairs", align_bytes=64)
+        up = [keep.tile([P, U], F32, name="up%d" % t) for t in range(PACK)]
         w2_codes = keep.tile([P, N], U32, name="w2_codes", align_bytes=64)
         w2_plane = keep.tile([P, N], U8, name="w2_plane", align_bytes=64)
 
         x_by_slot = xT.rearrange("(p j) c -> p j c", j=PACK)
         w1_by_slot = w1.rearrange("(p j) c -> p j c", j=PACK)
         skip_by_slot = skip.rearrange("(p t) v -> p t v", t=PACK)
+
+        def by_group(ap):
+            return ap.rearrange("p (g v) -> p g v", v=GROUP)
 
         nc.sync.dma_start(out=x_rows[0][:], in_=x_by_slot[:, 0, :])
         nc.sync.dma_start(offs_sb[:], offs)
@@ -68,21 +73,25 @@ def tile_picked_unet_relu_e_kernel(tc, xT, w1, w2_words, w2_scales, skip, offs, 
         nc.vector.memset(w2_plane[:].bitcast(I32), 0)
         for q in range(4):
             nc.sync.dma_start(out=w2_plane[32 * q : 32 * q + 4, :].bitcast(I32), in_=w2_scales[0, 4 * q : 4 * q + 4, :].bitcast(I32))
-        nc.sync.dma_start(out=skip_rows[0][:], in_=skip_by_slot[:, 0:2, :])
-        nc.sync.dma_start(out=skip_rows[1][:], in_=skip_by_slot[:, 2:4, :])
+        nc.sync.dma_start(out=skip0[:], in_=skip_by_slot[:, 0, OWN:])
+        nc.sync.dma_start(out=pairs[:, :, 1, :], in_=by_group(skip_by_slot[:, 1, OWN:]))
+        nc.sync.dma_start(out=skip01[:], in_=skip_by_slot[:, 0:2, :OWN])
+        nc.sync.dma_start(out=skip23[:], in_=skip_by_slot[:, 2:4, :])
 
         for t in range(PACK):
             nc.vector.memset(up[t][:], 0.0)
 
         picked = keep.tile([P, S, PACK], BF16, name="picked", align_bytes=64)
-        for j in range(PACK - 1):
+        late_rows = keep.tile([P, 2, HALF], BF16, name="late_rows", align_bytes=64)
+        for j in range(2):
             nc.vector.tensor_copy(picked[:, :, j], x_rows[j][:].indirect(offs_sb[:]))
-        for first in (0, HALF):
-            nc.vector.tensor_copy(picked[:, first : first + HALF, PACK - 1],
-                                  x_rows[PACK - 1][:].indirect(offs_sb[:, first // LIST_ROWS : (first + HALF) // LIST_ROWS]))
+        for j in range(2, PACK):
+            nc.scalar.activation(late_rows[:, j - 2, :], x_rows[j][:].indirect(offs_sb[:, HALF // LIST_ROWS :]), COPY)
+            nc.vector.tensor_copy(picked[:, :HALF, j], x_rows[j][:].indirect(offs_sb[:, : HALF // LIST_ROWS]))
+        nc.vector.tensor_copy(picked[:, HALF:, 2:PACK], late_rows[:].rearrange("p j s -> p s j"))
         x_codes = keep.tile([P, S], U32, name="x_codes", align_bytes=64)
         x_plane = keep.tile([P, S], U8, name="x_plane", align_bytes=64)
-        w1_pair = [keep.tile([P, 2, P, PACK], BF16, name="w1_pair%d" % h, align_bytes=64) for h in range(2)]
+        w1_dealt = keep.tile([P, PACK, P, PACK], BF16, name="w1_dealt", align_bytes=64)
         w1_codes = keep.tile([P, H], U32, name="w1_codes", align_bytes=64)
         w1_plane = keep.tile([P, H], U8, name="w1_plane", align_bytes=64)
         hidden = [keep.tile([P, S], F32, name="hidden%d" % t, tag="hidden%d" % t, align_bytes=64) for t in range(PACK)]
@@ -91,14 +100,14 @@ def tile_picked_unet_relu_e_kernel(tc, xT, w1, w2_words, w2_scales, skip, offs, 
             nc.vector.quantize_mx(out=x_codes[:, cols].bitcast(FP8X4), scales=x_plane[:, cols],
                                   in_=picked[:, cols, :].rearrange("p s j -> p (s j)"))
 
-        def deal(copy, u, h):
-            copy(w1_pair[h][:, :, :, 2 * u : 2 * u + 2].rearrange("p t m j -> p m t j"),
-                 w1_rows[u][:].rearrange("p j (m t) -> p m t j", t=PACK)[:, :, 2 * h : 2 * h + 2, :])
+        def deal(copy, u, tiles):
+            copy(w1_dealt[:, tiles, :, 2 * u : 2 * u + 2].rearrange("p t m j -> p m t j"),
+                 w1_rows[u][:].rearrange("p j (m t) -> p m t j", t=PACK)[:, :, tiles, :])
 
-        def quantize_w1(h):
-            cols = slice(2 * h * P, (2 * h + 2) * P)
+        def quantize_w1(tiles):
+            cols = slice(tiles.start * P, tiles.stop * P)
             nc.vector.quantize_mx(out=w1_codes[:, cols].bitcast(FP8X4), scales=w1_plane[:, cols],
-                                  in_=w1_pair[h][:].rearrange("p t m j -> p (t m j)"))
+                                  in_=w1_dealt[:, tiles, :, :].rearrange("p t m j -> p (t m j)"))
 
         def bank(b):
             return psum.tile([P, BANK], F32, name="bank", tag="bank%d" % b)
@@ -109,74 +118,78 @@ def tile_picked_unet_relu_e_kernel(tc, xT, w1, w2_words, w2_scales, skip, offs, 
             for cols in pieces:
                 nc.tensor.matmul_mx(out=acc[:, cols], lhsT=w1_codes[:, mine].bitcast(FP8X4), lhsT_scale=w1_plane[:, mine],
                                     rhs=x_codes[:, cols].bitcast(FP8X4), rhs_scale=x_plane[:, cols], start=True, stop=True)
-            return acc
+            cols = slice(pieces[0].start, pieces[-1].stop)
+            nc.scalar.activation(hidden[t][:, cols], acc[:, cols], RELU)
 
         def entries(cols):
             return cell_sb[:, cols.start // LIST_ROWS : cols.stop // LIST_ROWS]
 
-        def relu_on_scalar(values, acc, cols):
-            nc.scalar.activation(values, acc[:, cols], RELU)
+        def scatter_on_scalar(t, cols):
+            nc.scalar.activation(up[t][:].indirect(entries(cols)), hidden[t][:, cols], COPY)
 
-        def relu_on_vector(values, acc, cols):
-            nc.vector.tensor_scalar_max(values, acc[:, cols], 0.0)
-
-        def scatter_on_scalar(t, cols, values):
-            nc.scalar.activation(up[t][:].indirect(entries(cols)), values, COPY)
-
-        def scatter_on_vector(t, cols, values):
-            nc.vector.tensor_copy(up[t][:].indirect(entries(cols)), values)
-
-        def by_group(ap):
-            return ap.rearrange("p (g v) -> p g v", v=GROUP)
+        def scatter_on_vector(t, cols):
+            nc.vector.tensor_copy(up[t][:].indirect(entries(cols)), hidden[t][:, cols])
 
         def pair_rows(cols):
-            return pairs[:, cols.start // GROUP : cols.stop // GROUP, :, :]
+            return pairs[:, (cols.start - OWN) // GROUP : (cols.stop - OWN) // GROUP, :, :]
 
-        def add_skip(engine, t, cols):
+        def add_skip(engine, t, cols, addend):
             words = pair_rows(cols)[:, :, t // 2, :]
             halves = words.bitcast(BF16).rearrange("p g (v e) -> p g v e", e=2)[:, :, :, t % 2]
-            engine.tensor_tensor(halves, by_group(up[t][:, cols]), by_group(skip_rows[t // 2][:, t % 2, cols]), ADD)
+            engine.tensor_tensor(halves, by_group(up[t][:, cols]), addend, ADD)
 
-        lead = slice(0, LEAD)
-        second = slice(LEAD, HALF)
         early = slice(0, HALF)
         late = slice(HALF, S)
-        rest = slice(LEAD, S)
         whole = slice(0, S)
+        lead = slice(0, LEAD)
+        rest = slice(LEAD, S)
 
-        deal(nc.scalar.copy, 0, 0)
-        deal(nc.scalar.copy, 0, 1)
+        deal(nc.scalar.copy, 0, slice(0, 2))
+        deal(nc.scalar.copy, 0, slice(2, 4))
         quantize_x(early)
         quantize_x(late)
-        deal(nc.vector.tensor_copy, 1, 0)
-        deal(nc.scalar.copy, 1, 1)
-        quantize_w1(0)
-        relu_on_vector(hidden[0][:, lead], first_layer(0, [lead], 0), lead)
-        quantize_w1(1)
-        scatter_on_vector(0, lead, hidden[0][:, lead])
-        relu_on_scalar(hidden[1][:, early], first_layer(1, [early], 1), early)
-        relu_on_scalar(hidden[0][:, rest], first_layer(0, [second, late], 2), rest)
-        relu_on_scalar(hidden[1][:, late], first_layer(1, [late], 3), late)
-        scatter_on_scalar(0, rest, hidden[0][:, rest])
+        deal(nc.vector.tensor_copy, 1, slice(0, 1))
+        deal(nc.vector.tensor_copy, 1, slice(1, 2))
+        deal(nc.scalar.copy, 1, slice(2, 4))
+        quantize_w1(slice(0, 1))
+        quantize_w1(slice(1, 2))
+        quantize_w1(slice(2, 4))
+        first_layer(0, [lead], 0)
+        scatter_on_vector(0, lead)
+        first_layer(1, [early], 1)
+        first_layer(0, [slice(LEAD, HALF), late], 2)
+        first_layer(1, [late], 3)
+        scatter_on_scalar(0, rest)
         for cols in (early, late):
-            scatter_on_vector(1, cols, hidden[1][:, cols])
-        for t in (2, 3):
-            relu_on_scalar(hidden[t][:], first_layer(t, [whole], 2 + t), whole)
-        scatter_on_vector(2, whole, hidden[2][:])
+            scatter_on_vector(1, cols)
+        first_layer(2, [whole], 2)
+        first_layer(3, [whole], 3)
+        scatter_on_vector(2, whole)
         for cols in (early, late):
-            scatter_on_scalar(3, cols, hidden[3][:, cols])
-        for t in (0, 1):
-            add_skip(nc.gpsimd, t, slice(0, GPSIMD_CELLS))
+            scatter_on_scalar(3, cols)
+        add_skip(nc.gpsimd, 0, slice(OWN, U), by_group(skip0[:]))
+        add_skip(nc.gpsimd, 1, slice(OWN, U), pairs[:, :, 1, :])
+        own_sums = up[1][:, OWN : 3 * OWN].bitcast(BF16).rearrange("p (t v) -> p t v", t=PACK)
 
         out_by_tile = out.rearrange("(a p) v -> p a v", p=P)
         spans = spans_of(CHUNKS)
-        z = [keep.tile([P, 2 * width], F32, name="z%d" % c, tag="z%d" % c, align_bytes=64) for c, width in enumerate(CHUNKS)]
+        z = [keep.tile([P, 2 * width], U32, name="z%d" % c, align_bytes=64) for c, width in enumerate(CHUNKS)]
         z_codes = [keep.tile([P, width], U32, name="z_codes%d" % c, align_bytes=64) for c, width in enumerate(CHUNKS)]
         z_plane = [keep.tile([P, width], U8, name="z_plane%d" % c, align_bytes=64) for c, width in enumerate(CHUNKS)]
 
-        def weave(c):
-            rows = pair_rows(spans[c])
-            nc.scalar.copy(z[c][:].bitcast(U32).rearrange("p (g v u) -> p g v u", v=GROUP, u=2), rows.bitcast(U32).rearrange("p g u v -> p g v u"))
+        def add_late(t, first, last):
+            cols = slice(spans[first].start, spans[last].stop)
+            add_skip(nc.vector, t, cols, by_group(skip23[:, t - 2, cols]))
+
+        def add_own(t):
+            rows = skip01 if t < 2 else skip23
+            nc.vector.tensor_tensor(own_sums[:, t, :], up[t][:, :OWN], rows[:, t % 2, :OWN], ADD)
+
+        def weave_own(c, copy):
+            copy(z[c][:].bitcast(BF16).rearrange("p (g v t) -> p g t v", v=RUN, t=PACK), own_sums[:, :, spans[c]].rearrange("p t (g v) -> p g t v", v=RUN))
+
+        def weave(c, copy):
+            copy(z[c][:].rearrange("p (g v u) -> p g v u", v=GROUP, u=2), pair_rows(spans[c]).bitcast(U32).rearrange("p g u v -> p g v u"))
 
         def quantize_z(c):
             nc.vector.quantize_mx(out=z_codes[c][:].bitcast(FP8X4), scales=z_plane[c][:], in_=z[c][:].bitcast(BF16))
@@ -189,48 +202,42 @@ def tile_picked_unet_relu_e_kernel(tc, xT, w1, w2_words, w2_scales, skip, offs, 
                                     rhs_scale=z_plane[c][:, cols], start=True, stop=True)
 
         def finish(c, b, copy):
-            cols = spans[c]
-            width = cols.stop - cols.start
+            width = CHUNKS[c]
             acc = bank(b)
             for a in range(N // P):
                 second_layer(acc[:, a * width : (a + 1) * width], a, c)
             result = keep.tile([P, N // P, width], F32, name="result%d" % c)
             copy(result[:].rearrange("p a v -> p (a v)"), acc[:, : 2 * width])
-            nc.sync.dma_start(out=out_by_tile[:, :, cols], in_=result[:])
+            nc.sync.dma_start(out=out_by_tile[:, :, spans[c]], in_=result[:])
 
         def finish_split(c, banks, copies):
-            cols = spans[c]
-            width = cols.stop - cols.start
+            width = CHUNKS[c]
             for a, copy in enumerate(copies):
                 acc = bank(banks[a])
                 second_layer(acc[:, :width], a, c)
                 result = keep.tile([P, width], F32, name="result%d_%d" % (c, a))
                 copy(result[:], acc[:, :width])
-                nc.sync.dma_start(out=out_by_tile[:, a, cols], in_=result[:])
+                nc.sync.dma_start(out=out_by_tile[:, a, spans[c]], in_=result[:])
 
-        def add_all(c, copy):
-            cols = spans[c]
-            sums = keep.tile([P, PACK, CHUNKS[c]], F32, name="sums%d" % c, tag="z%d" % (c - 3), align_bytes=64)
-            for t in range(PACK):
-                nc.vector.tensor_tensor(sums[:, t, :], up[t][:, cols], skip_rows[t // 2][:, t % 2, cols], ADD)
-            copy(z[c][:].bitcast(BF16).rearrange("p (g v t) -> p g t v", v=4, t=PACK), sums[:].rearrange("p t (g v) -> p g t v", v=4))
-
-        add_skip(nc.vector, 2, slice(0, FRONT))
-        for c in range(2):
-            add_skip(nc.vector, 3, spans[c])
-            weave(c)
-        for t in (2, 3):
-            add_skip(nc.vector, t, spans[2])
-        weave(2)
-        quantize_z(0)
-        quantize_z(1)
-        finish(0, 0, nc.scalar.copy)
-        add_all(3, nc.scalar.copy)
-        finish(1, 1, nc.scalar.copy)
+        add_late(2, 2, 3)
+        add_late(3, 2, 2)
+        weave(2, nc.scalar.copy)
+        add_late(3, 3, 3)
+        weave(3, nc.scalar.copy)
+        add_late(2, 4, 4)
         quantize_z(2)
-        add_all(4, nc.vector.tensor_copy)
-        finish_split(2, (2, 3), (nc.scalar.copy, nc.scalar.copy))
+        add_late(3, 4, 4)
+        weave(4, nc.scalar.copy)
         quantize_z(3)
+        finish(2, 4, nc.scalar.copy)
+        for t in range(PACK):
+            add_own(t)
+        finish(3, 5, nc.scalar.copy)
+        weave_own(0, nc.scalar.copy)
         quantize_z(4)
-        finish(3, 4, nc.vector.tensor_copy)
-        finish_split(4, (6, 7), (nc.scalar.copy, nc.vector.tensor_copy))
+        weave_own(1, nc.vector.tensor_copy)
+        finish_split(4, (6, 7), (nc.scalar.copy, nc.scalar.copy))
+        quantize_z(1)
+        quantize_z(0)
+        finish(1, 0, nc.vector.tensor_copy)
+        finish_split(0, (1, 2), (nc.scalar.copy, nc.vector.tensor_copy))

@@ -21,11 +21,10 @@ PACK = 4
 BANK = 512
 LIST_ROWS = 16
 HALF = S // 2
-GROUP = 128
 RUN = 8
 OWN = 256
 LEAD = 128
-CHUNKS = (128, 128, 128, 256, 384)
+CHUNKS = (128, 128, 128, 256, 256, 128)
 
 
 def spans_of(widths):
@@ -50,7 +49,7 @@ def tile_picked_unet_relu_e_kernel(tc, xT, w1, w2_words, w2_scales, skip, offs, 
         skip23 = keep.tile([P, 2, U], F32, name="skip23")
         skip0 = keep.tile([P, U - OWN], F32, name="skip0")
         skip01 = keep.tile([P, 2, OWN], F32, name="skip01")
-        pairs = keep.tile([P, (U - OWN) // GROUP, 2, GROUP], F32, name="pairs", align_bytes=64)
+        sums = keep.tile([P, PACK, U - OWN], BF16, name="sums", align_bytes=64)
         up = [keep.tile([P, U], F32, name="up%d" % t) for t in range(PACK)]
         w2_codes = keep.tile([P, N], U32, name="w2_codes", align_bytes=64)
         w2_plane = keep.tile([P, N], U8, name="w2_plane", align_bytes=64)
@@ -58,9 +57,6 @@ def tile_picked_unet_relu_e_kernel(tc, xT, w1, w2_words, w2_scales, skip, offs, 
         x_by_slot = xT.rearrange("(p j) c -> p j c", j=PACK)
         w1_by_slot = w1.rearrange("(p j) c -> p j c", j=PACK)
         skip_by_slot = skip.rearrange("(p t) v -> p t v", t=PACK)
-
-        def by_group(ap):
-            return ap.rearrange("p (g v) -> p g v", v=GROUP)
 
         nc.sync.dma_start(out=x_rows[0][:], in_=x_by_slot[:, 0, :])
         nc.sync.dma_start(offs_sb[:], offs)
@@ -74,7 +70,8 @@ def tile_picked_unet_relu_e_kernel(tc, xT, w1, w2_words, w2_scales, skip, offs, 
         for q in range(4):
             nc.sync.dma_start(out=w2_plane[32 * q : 32 * q + 4, :].bitcast(I32), in_=w2_scales[0, 4 * q : 4 * q + 4, :].bitcast(I32))
         nc.sync.dma_start(out=skip0[:], in_=skip_by_slot[:, 0, OWN:])
-        nc.sync.dma_start(out=pairs[:, :, 1, :], in_=by_group(skip_by_slot[:, 1, OWN:]))
+        skip1 = sums[:, 2:4, :].rearrange("p t v -> p (t v)").bitcast(F32)
+        nc.sync.dma_start(out=skip1, in_=skip_by_slot[:, 1, OWN:])
         nc.sync.dma_start(out=skip01[:], in_=skip_by_slot[:, 0:2, :OWN])
         nc.sync.dma_start(out=skip23[:], in_=skip_by_slot[:, 2:4, :])
 
@@ -130,13 +127,10 @@ def tile_picked_unet_relu_e_kernel(tc, xT, w1, w2_words, w2_scales, skip, offs, 
         def scatter_on_vector(t, cols):
             nc.vector.tensor_copy(up[t][:].indirect(entries(cols)), hidden[t][:, cols])
 
-        def pair_rows(cols):
-            return pairs[:, (cols.start - OWN) // GROUP : (cols.stop - OWN) // GROUP, :, :]
-
-        def add_skip(engine, t, cols, addend):
-            words = pair_rows(cols)[:, :, t // 2, :]
-            halves = words.bitcast(BF16).rearrange("p g (v e) -> p g v e", e=2)[:, :, :, t % 2]
-            engine.tensor_tensor(halves, by_group(up[t][:, cols]), addend, ADD)
+        def sum_rows(cols):
+            if cols.start < OWN:
+                return own_sums[:, :, cols]
+            return sums[:, :, cols.start - OWN : cols.stop - OWN]
 
         early = slice(0, HALF)
         late = slice(HALF, S)
@@ -167,32 +161,26 @@ def tile_picked_unet_relu_e_kernel(tc, xT, w1, w2_words, w2_scales, skip, offs, 
         scatter_on_vector(2, whole)
         for cols in (early, late):
             scatter_on_scalar(3, cols)
-        add_skip(nc.gpsimd, 0, slice(OWN, U), by_group(skip0[:]))
-        add_skip(nc.gpsimd, 1, slice(OWN, U), pairs[:, :, 1, :])
+        nc.gpsimd.tensor_tensor(sums[:, 0, :], up[0][:, OWN:], skip0[:], ADD)
+        nc.gpsimd.tensor_tensor(sums[:, 1, :], up[1][:, OWN:], skip1, ADD)
         own_sums = up[1][:, OWN : 3 * OWN].bitcast(BF16).rearrange("p (t v) -> p t v", t=PACK)
 
         out_by_tile = out.rearrange("(a p) v -> p a v", p=P)
         spans = spans_of(CHUNKS)
-        z = [keep.tile([P, 2 * width], U32, name="z%d" % c, align_bytes=64) for c, width in enumerate(CHUNKS)]
+        z = [keep.tile([P, PACK * width], BF16, name="z%d" % c, align_bytes=64) for c, width in enumerate(CHUNKS)]
         z_codes = [keep.tile([P, width], U32, name="z_codes%d" % c, align_bytes=64) for c, width in enumerate(CHUNKS)]
         z_plane = [keep.tile([P, width], U8, name="z_plane%d" % c, align_bytes=64) for c, width in enumerate(CHUNKS)]
 
         def add_late(t, first, last):
             cols = slice(spans[first].start, spans[last].stop)
-            add_skip(nc.vector, t, cols, by_group(skip23[:, t - 2, cols]))
-
-        def add_own(t):
             rows = skip01 if t < 2 else skip23
-            nc.vector.tensor_tensor(own_sums[:, t, :], up[t][:, :OWN], rows[:, t % 2, :OWN], ADD)
-
-        def weave_own(c, copy):
-            copy(z[c][:].bitcast(BF16).rearrange("p (g v t) -> p g t v", v=RUN, t=PACK), own_sums[:, :, spans[c]].rearrange("p t (g v) -> p g t v", v=RUN))
+            nc.vector.tensor_tensor(sum_rows(cols)[:, t, :], up[t][:, cols], rows[:, t % 2, cols], ADD)
 
         def weave(c, copy):
-            copy(z[c][:].rearrange("p (g v u) -> p g v u", v=GROUP, u=2), pair_rows(spans[c]).bitcast(U32).rearrange("p g u v -> p g v u"))
+            copy(z[c][:].rearrange("p (g v t) -> p g t v", v=RUN, t=PACK), sum_rows(spans[c]).rearrange("p t (g v) -> p g t v", v=RUN))
 
         def quantize_z(c):
-            nc.vector.quantize_mx(out=z_codes[c][:].bitcast(FP8X4), scales=z_plane[c][:], in_=z[c][:].bitcast(BF16))
+            nc.vector.quantize_mx(out=z_codes[c][:].bitcast(FP8X4), scales=z_plane[c][:], in_=z[c][:])
 
         def second_layer(acc, a, c):
             for first in range(0, CHUNKS[c], 2 * P):
@@ -219,25 +207,28 @@ def tile_picked_unet_relu_e_kernel(tc, xT, w1, w2_words, w2_scales, skip, offs, 
                 copy(result[:], acc[:, :width])
                 nc.sync.dma_start(out=out_by_tile[:, a, spans[c]], in_=result[:])
 
-        add_late(2, 2, 3)
-        add_late(3, 2, 2)
+        add_late(2, 2, 5)
+        add_late(3, 2, 3)
         weave(2, nc.scalar.copy)
-        add_late(3, 3, 3)
-        weave(3, nc.scalar.copy)
-        add_late(2, 4, 4)
-        quantize_z(2)
-        add_late(3, 4, 4)
+        add_late(3, 4, 5)
         weave(4, nc.scalar.copy)
+        weave(3, nc.vector.tensor_copy)
+        quantize_z(2)
         quantize_z(3)
         finish(2, 4, nc.scalar.copy)
-        for t in range(PACK):
-            add_own(t)
         finish(3, 5, nc.scalar.copy)
-        weave_own(0, nc.scalar.copy)
+        add_late(0, 0, 1)
+        add_late(1, 0, 1)
         quantize_z(4)
-        weave_own(1, nc.vector.tensor_copy)
-        finish_split(4, (6, 7), (nc.scalar.copy, nc.scalar.copy))
+        add_late(2, 0, 1)
+        add_late(3, 0, 1)
+        weave(0, nc.scalar.copy)
+        weave(5, nc.vector.tensor_copy)
+        weave(1, nc.vector.tensor_copy)
+        quantize_z(5)
         quantize_z(1)
         quantize_z(0)
+        finish(4, 6, nc.scalar.copy)
+        finish(5, 7, nc.scalar.copy)
         finish(1, 0, nc.vector.tensor_copy)
         finish_split(0, (1, 2), (nc.scalar.copy, nc.vector.tensor_copy))

@@ -216,19 +216,19 @@ def tile_picked_unet_relu_e_kernel(tc, xT, w1, w2_words, w2_scales, skip, offs, 
         quantize_z(2)
         quantize_z(3)
         finish(2, 4, nc.scalar.copy)
-        finish(3, 5, nc.scalar.copy)
+        finish_split(3, (5, 6), (nc.scalar.copy, nc.scalar.copy))
         add_late(0, 0, 1)
-        add_late(1, 0, 1)
         quantize_z(4)
+        finish_split(4, (7, 0), (nc.scalar.copy, nc.scalar.copy))
+        add_late(1, 0, 1)
+        weave(5, nc.vector.tensor_copy)
         add_late(2, 0, 1)
         add_late(3, 0, 1)
-        weave(0, nc.scalar.copy)
-        weave(5, nc.vector.tensor_copy)
-        weave(1, nc.vector.tensor_copy)
         quantize_z(5)
-        quantize_z(1)
+        finish(5, 1, nc.scalar.copy)
+        weave(0, nc.vector.tensor_copy)
+        weave(1, nc.vector.tensor_copy)
         quantize_z(0)
-        finish(4, 6, nc.scalar.copy)
-        finish(5, 7, nc.scalar.copy)
-        finish(1, 0, nc.vector.tensor_copy)
-        finish_split(0, (1, 2), (nc.scalar.copy, nc.vector.tensor_copy))
+        quantize_z(1)
+        finish(0, 2, nc.scalar.copy)
+        finish_split(1, (3, 4), (nc.vector.tensor_copy, nc.scalar.copy))

@@ -47,7 +47,7 @@ def tile_picked_unet_relu_e_kernel(tc, xT, w1, w2_words, w2_scales, skip, offs, 
         x_rows = [keep.tile([P, T], F32, name="x_rows%d" % j) for j in range(PACK)]
         w1_rows = [keep.tile([P, 2, H], F32, name="w1_rows%d" % u) for u in range(2)]
         skip23 = keep.tile([P, 2, U], F32, name="skip23")
-        skip0 = keep.tile([P, U - OWN], F32, name="skip0")
+        skip1 = keep.tile([P, U - OWN], F32, name="skip1")
         skip01 = keep.tile([P, 2, OWN], F32, name="skip01")
         sums = keep.tile([P, PACK, U - OWN], BF16, name="sums", align_bytes=64)
         up = [keep.tile([P, U], F32, name="up%d" % t) for t in range(PACK)]
@@ -69,9 +69,9 @@ def tile_picked_unet_relu_e_kernel(tc, xT, w1, w2_words, w2_scales, skip, offs, 
         nc.vector.memset(w2_plane[:].bitcast(I32), 0)
         for q in range(4):
             nc.sync.dma_start(out=w2_plane[32 * q : 32 * q + 4, :].bitcast(I32), in_=w2_scales[0, 4 * q : 4 * q + 4, :].bitcast(I32))
-        nc.sync.dma_start(out=skip0[:], in_=skip_by_slot[:, 0, OWN:])
-        skip1 = sums[:, 2:4, :].rearrange("p t v -> p (t v)").bitcast(F32)
-        nc.sync.dma_start(out=skip1, in_=skip_by_slot[:, 1, OWN:])
+        skip0 = sums[:, 2:4, :].rearrange("p t v -> p (t v)").bitcast(F32)
+        nc.sync.dma_start(out=skip0, in_=skip_by_slot[:, 0, OWN:])
+        nc.sync.dma_start(out=skip1[:], in_=skip_by_slot[:, 1, OWN:])
         nc.sync.dma_start(out=skip01[:], in_=skip_by_slot[:, 0:2, :OWN])
         nc.sync.dma_start(out=skip23[:], in_=skip_by_slot[:, 2:4, :])
 
@@ -161,8 +161,8 @@ def tile_picked_unet_relu_e_kernel(tc, xT, w1, w2_words, w2_scales, skip, offs, 
         scatter_on_vector(2, whole)
         for cols in (early, late):
             scatter_on_scalar(3, cols)
-        nc.gpsimd.tensor_tensor(sums[:, 0, :], up[0][:, OWN:], skip0[:], ADD)
-        nc.gpsimd.tensor_tensor(sums[:, 1, :], up[1][:, OWN:], skip1, ADD)
+        nc.gpsimd.tensor_tensor(sums[:, 0, :], up[0][:, OWN:], skip0, ADD)
+        nc.gpsimd.tensor_tensor(sums[:, 1, :], up[1][:, OWN:], skip1[:], ADD)
         own_sums = up[1][:, OWN : 3 * OWN].bitcast(BF16).rearrange("p (t v) -> p t v", t=PACK)
 
         out_by_tile = out.rearrange("(a p) v -> p a v", p=P)

from contextlib import ExitStack

import concourse.mybir as mybir

K, T, S, H, N, U = 512, 2048, 512, 512, 256, 1024
FLOPS = 2 * K * H * S + 2 * H * N * U

F32 = mybir.dt.float32
BF16 = mybir.dt.bfloat16
I32 = mybir.dt.int32
U32 = mybir.dt.uint32
U16 = mybir.dt.uint16
U8 = mybir.dt.uint8
FP8X4 = mybir.dt.float8_e4m3fn_x4
ADD = mybir.AluOpType.add
RELU = mybir.ActivationFunctionType.Relu
COPY = mybir.ActivationFunctionType.Copy

P = 128
PACK = 4
BANK = 512
LIST_ROWS = 16
HALF = S // 2
RUN = 8
OWN = 256
LEAD = 128
CHUNKS = (128, 128, 128, 256, 256, 128)


def spans_of(widths):
    spans = []
    start = 0
    for width in widths:
        spans.append(slice(start, start + width))
        start = start + width
    return spans


def tile_picked_unet_relu_e_kernel(tc, xT, w1, w2_words, w2_scales, skip, offs, cell, out):
    nc = tc.nc
    with ExitStack() as ctx:
        keep = ctx.enter_context(tc.tile_pool(name="keep", bufs=1))
        psum = ctx.enter_context(tc.psum_pool(name="psum", bufs=1))

        offs_sb = keep.tile([P, S // LIST_ROWS], U16, name="offs_sb")
        cell_sb = keep.tile([P, S // LIST_ROWS], U16, name="cell_sb")
        x_rows = [keep.tile([P, T], F32, name="x_rows%d" % j) for j in range(PACK)]
        w1_rows = [keep.tile([P, 2, H], F32, name="w1_rows%d" % u) for u in range(2)]
        skip23 = keep.tile([P, 2, U], F32, name="skip23")
        skip1 = keep.tile([P, U - OWN], F32, name="skip1")
        skip01 = keep.tile([P, 2, OWN], F32, name="skip01")
        sums = keep.tile([P, PACK, U - OWN], BF16, name="sums", align_bytes=64)
        up = [keep.tile([P, U], F32, name="up%d" % t) for t in range(PACK)]
        w2_codes = keep.tile([P, N], U32, name="w2_codes", align_bytes=64)
        w2_plane = keep.tile([P, N], U8, name="w2_plane", align_bytes=64)

        x_by_slot = xT.rearrange("(p j) c -> p j c", j=PACK)
        w1_by_slot = w1.rearrange("(p j) c -> p j c", j=PACK)
        skip_by_slot = skip.rearrange("(p t) v -> p t v", t=PACK)

        nc.sync.dma_start(out=x_rows[0][:], in_=x_by_slot[:, 0, :])
        nc.sync.dma_start(offs_sb[:], offs)
        for j in range(1, PACK):
            nc.sync.dma_start(out=x_rows[j][:], in_=x_by_slot[:, j, :])
        for u in range(2):
            nc.sync.dma_start(out=w1_rows[u][:], in_=w1_by_slot[:, 2 * u : 2 * u + 2, :])
        nc.sync.dma_start(cell_sb[:], cell)
        nc.sync.dma_start(out=w2_codes[:].bitcast(I32), in_=w2_words[0].rearrange("p n t -> p (n t)").bitcast(I32))
        nc.vector.memset(w2_plane[:].bitcast(I32), 0)
        for q in range(4):
            nc.sync.dma_start(out=w2_plane[32 * q : 32 * q + 4, :].bitcast(I32), in_=w2_scales[0, 4 * q : 4 * q + 4, :].bitcast(I32))
        skip0 = sums[:, 2:4, :].rearrange("p t v -> p (t v)").bitcast(F32)
        nc.sync.dma_start(out=skip0, in_=skip_by_slot[:, 0, OWN:])
        nc.sync.dma_start(out=skip1[:], in_=skip_by_slot[:, 1, OWN:])
        nc.sync.dma_start(out=skip01[:], in_=skip_by_slot[:, 0:2, :OWN])
        nc.sync.dma_start(out=skip23[:], in_=skip_by_slot[:, 2:4, :])

        for t in range(PACK):
            nc.vector.memset(up[t][:], 0.0)

        picked = keep.tile([P, S, PACK], BF16, name="picked", align_bytes=64)
        late_rows = keep.tile([P, 2, HALF], BF16, name="late_rows", align_bytes=64)
        for j in range(2):
            nc.vector.tensor_copy(picked[:, :, j], x_rows[j][:].indirect(offs_sb[:]))
        for j in range(2, PACK):
            nc.scalar.activation(late_rows[:, j - 2, :], x_rows[j][:].indirect(offs_sb[:, HALF // LIST_ROWS :]), COPY)
            nc.vector.tensor_copy(picked[:, :HALF, j], x_rows[j][:].indirect(offs_sb[:, : HALF // LIST_ROWS]))
        nc.vector.tensor_copy(picked[:, HALF:, 2:PACK], late_rows[:].rearrange("p j s -> p s j"))
        x_codes = keep.tile([P, S], U32, name="x_codes", align_bytes=64)
        x_plane = keep.tile([P, S], U8, name="x_plane", align_bytes=64)
        w1_dealt = keep.tile([P, PACK, P, PACK], BF16, name="w1_dealt", align_bytes=64)
        w1_codes = keep.tile([P, H], U32, name="w1_codes", align_bytes=64)
        w1_plane = keep.tile([P, H], U8, name="w1_plane", align_bytes=64)
        hidden = [keep.tile([P, S], F32, name="hidden%d" % t, tag="hidden%d" % t, align_bytes=64) for t in range(PACK)]

        def quantize_x(cols):
            nc.vector.quantize_mx(out=x_codes[:, cols].bitcast(FP8X4), scales=x_plane[:, cols],
                                  in_=picked[:, cols, :].rearrange("p s j -> p (s j)"))

        def deal(copy, u, tiles):
            copy(w1_dealt[:, tiles, :, 2 * u : 2 * u + 2].rearrange("p t m j -> p m t j"),
                 w1_rows[u][:].rearrange("p j (m t) -> p m t j", t=PACK)[:, :, tiles, :])

        def quantize_w1(tiles):
            cols = slice(tiles.start * P, tiles.stop * P)
            nc.vector.quantize_mx(out=w1_codes[:, cols].bitcast(FP8X4), scales=w1_plane[:, cols],
                                  in_=w1_dealt[:, tiles, :, :].rearrange("p t m j -> p (t m j)"))

        def bank(b):
            return psum.tile([P, BANK], F32, name="bank", tag="bank%d" % b)

        def first_layer(t, pieces, b):
            acc = bank(b)
            mine = slice(t * P, (t + 1) * P)
            for cols in pieces:
                nc.tensor.matmul_mx(out=acc[:, cols], lhsT=w1_codes[:, mine].bitcast(FP8X4), lhsT_scale=w1_plane[:, mine],
                                    rhs=x_codes[:, cols].bitcast(FP8X4), rhs_scale=x_plane[:, cols], start=True, stop=True)
            cols = slice(pieces[0].start, pieces[-1].stop)
            nc.scalar.activation(hidden[t][:, cols], acc[:, cols], RELU)

        def entries(cols):
            return cell_sb[:, cols.start // LIST_ROWS : cols.stop // LIST_ROWS]

        def scatter_on_scalar(t, cols):
            nc.scalar.activation(up[t][:].indirect(entries(cols)), hidden[t][:, cols], COPY)

        def scatter_on_vector(t, cols):
            nc.vector.tensor_copy(up[t][:].indirect(entries(cols)), hidden[t][:, cols])

        def sum_rows(cols):
            if cols.start < OWN:
                return own_sums[:, :, cols]
            return sums[:, :, cols.start - OWN : cols.stop - OWN]

        early = slice(0, HALF)
        late = slice(HALF, S)
        whole = slice(0, S)
        lead = slice(0, LEAD)
        rest = slice(LEAD, S)

        deal(nc.scalar.copy, 0, slice(0, 2))
        deal(nc.scalar.copy, 0, slice(2, 4))
        quantize_x(early)
        quantize_x(late)
        deal(nc.vector.tensor_copy, 1, slice(0, 1))
        deal(nc.vector.tensor_copy, 1, slice(1, 2))
        deal(nc.scalar.copy, 1, slice(2, 4))
        quantize_w1(slice(0, 1))
        quantize_w1(slice(1, 2))
        quantize_w1(slice(2, 4))
        first_layer(0, [lead], 0)
        scatter_on_vector(0, lead)
        first_layer(1, [early], 1)
        first_layer(0, [slice(LEAD, HALF), late], 2)
        first_layer(1, [late], 3)
        scatter_on_scalar(0, rest)
        for cols in (early, late):
            scatter_on_vector(1, cols)
        first_layer(2, [whole], 2)
        first_layer(3, [whole], 3)
        scatter_on_vector(2, whole)
        for cols in (early, late):
            scatter_on_scalar(3, cols)
        nc.gpsimd.tensor_tensor(sums[:, 0, :], up[0][:, OWN:], skip0, ADD)
        nc.gpsimd.tensor_tensor(sums[:, 1, :], up[1][:, OWN:], skip1[:], ADD)
        own_sums = up[1][:, OWN : 3 * OWN].bitcast(BF16).rearrange("p (t v) -> p t v", t=PACK)

        out_by_tile = out.rearrange("(a p) v -> p a v", p=P)
        spans = spans_of(CHUNKS)
        z = [keep.tile([P, PACK * width], BF16, name="z%d" % c, align_bytes=64) for c, width in enumerate(CHUNKS)]
        z_codes = [keep.tile([P, width], U32, name="z_codes%d" % c, align_bytes=64) for c, width in enumerate(CHUNKS)]
        z_plane = [keep.tile([P, width], U8, name="z_plane%d" % c, align_bytes=64) for c, width in enumerate(CHUNKS)]

        def add_late(t, first, last):
            cols = slice(spans[first].start, spans[last].stop)
            rows = skip01 if t < 2 else skip23
            nc.vector.tensor_tensor(sum_rows(cols)[:, t, :], up[t][:, cols], rows[:, t % 2, cols], ADD)

        def weave(c, copy):
            copy(z[c][:].rearrange("p (g v t) -> p g t v", v=RUN, t=PACK), sum_rows(spans[c]).rearrange("p t (g v) -> p g t v", v=RUN))

        def quantize_z(c):
            nc.vector.quantize_mx(out=z_codes[c][:].bitcast(FP8X4), scales=z_plane[c][:], in_=z[c][:])

        def second_layer(acc, a, c):
            for first in range(0, CHUNKS[c], 2 * P):
                cols = slice(first, min(first + 2 * P, CHUNKS[c]))
                nc.tensor.matmul_mx(out=acc[:, cols], lhsT=w2_codes[:, a * P : (a + 1) * P].bitcast(FP8X4),
                                    lhsT_scale=w2_plane[:, a * P : (a + 1) * P], rhs=z_codes[c][:, cols].bitcast(FP8X4),
                                    rhs_scale=z_plane[c][:, cols], start=True, stop=True)

        def finish(c, b, copy):
            width = CHUNKS[c]
            acc = bank(b)
            for a in range(N // P):
                second_layer(acc[:, a * width : (a + 1) * width], a, c)
            result = keep.tile([P, N // P, width], F32, name="result%d" % c)
            copy(result[:].rearrange("p a v -> p (a v)"), acc[:, : 2 * width])
            nc.sync.dma_start(out=out_by_tile[:, :, spans[c]], in_=result[:])

        def finish_split(c, banks, copies):
            width = CHUNKS[c]
            for a, copy in enumerate(copies):
                acc = bank(banks[a])
                second_layer(acc[:, :width], a, c)
                result = keep.tile([P, width], F32, name="result%d_%d" % (c, a))
                copy(result[:], acc[:, :width])
                nc.sync.dma_start(out=out_by_tile[:, a, spans[c]], in_=result[:])

        add_late(2, 2, 5)
        add_late(3, 2, 3)
        weave(2, nc.scalar.copy)
        add_late(3, 4, 5)
        weave(4, nc.scalar.copy)
        weave(3, nc.vector.tensor_copy)
        quantize_z(2)
        quantize_z(3)
        finish(2, 4, nc.scalar.copy)
        finish_split(3, (5, 6), (nc.scalar.copy, nc.scalar.copy))
        add_late(0, 0, 1)
        quantize_z(4)
        finish_split(4, (7, 0), (nc.scalar.copy, nc.scalar.copy))
        add_late(1, 0, 1)
        weave(5, nc.vector.tensor_copy)
        add_late(2, 0, 1)
        add_late(3, 0, 1)
        quantize_z(5)
        finish(5, 1, nc.scalar.copy)
        weave(0, nc.vector.tensor_copy)
        weave(1, nc.vector.tensor_copy)
        quantize_z(0)
        quantize_z(1)
        finish(0, 2, nc.scalar.copy)
        finish_split(1, (3, 4), (nc.vector.tensor_copy, nc.scalar.copy))
